import numpy as np
import ml_dtypes


def mxq(x, axis, fmt="e4m3"):
    dtype, down = {"e4m3": (ml_dtypes.float8_e4m3fn, 7), "e5m2": (ml_dtypes.float8_e5m2, 14)}[fmt]
    v = np.moveaxis(np.asarray(x, np.float32).astype(ml_dtypes.bfloat16).astype(np.float64), axis, -1)
    blocks = v.reshape(v.shape[:-1] + (-1, 32))
    amax = np.abs(blocks).max(-1, keepdims=True)
    byte = np.maximum(np.where(amax > 0, np.frexp(amax)[1] - 1 + 127, 0) - down, 1)
    scale = np.exp2(byte - 127.0)
    codes = (blocks / scale).astype(np.float32).astype(dtype).astype(np.float64)
    return np.moveaxis((codes * scale).reshape(v.shape), -1, axis)


WIDE = False


def mx_kscale(k):
    if not WIDE:
        return np.ones(k)
    levels = np.array([10, -10, 5, -5, 0])
    if k % 512:
        return np.exp2(np.random.permutation(np.resize(levels, k // 32))).repeat(32)
    a = np.empty((k // 512, 16))
    for p in range(k // 512):
        a[p, :8] = np.random.permutation(np.resize(levels, 8))
        for g in range(8):
            far = levels[np.abs(levels - a[p, g]) >= 10]
            a[p, g + 8] = far[np.random.randint(len(far))]
    return np.exp2(a.ravel()).repeat(32)


BF16 = ml_dtypes.bfloat16


def bf(x):
    return np.asarray(x, np.float32).astype(BF16)


def f64(x):
    return np.asarray(x).astype(np.float64)

def planes(Y):
    n, m = Y.shape
    b = f64(bf(Y)).reshape(n // 32, 32, m)
    amax = np.abs(b).max(1)
    byte = np.clip(np.where(amax > 0, np.frexp(amax)[1] - 1 + 127 - 7, 1), 1, 254)
    codes = (b * np.exp2(127.0 - byte)[:, None, :]).reshape(n, m).astype(np.float32).astype(ml_dtypes.float8_e4m3fn).view(np.uint8)
    words = codes.reshape(n // 512, 128, 4, m).transpose(0, 1, 3, 2)
    return np.ascontiguousarray(words), np.ascontiguousarray(byte.astype(np.uint8).reshape(n // 512, 16, m))


B, D, R, E = 512, 1024, 512, 4


def setup_inputs():
    kd, kr = mx_kscale(D), mx_kscale(R)
    return {"x0": bf(np.random.standard_normal((B, D)) * kd),
            "xl": bf(np.random.standard_normal((B, D)) * kd),
            "v": bf(np.random.standard_normal((E, D, R)) / np.sqrt(D) / kd[:, None]),
            "s": bf((1.0 + 0.1 * np.random.standard_normal((E, R))) * kr),
            "u": bf(2.0 * np.random.standard_normal((E, R, D)) / np.sqrt(R) / kr[:, None]),
            "gw": bf(np.random.standard_normal((E, D)) / np.sqrt(D) / kd)}


def expert_outputs(xl, v, s, u):
    h = mxq(xl, 1, "e4m3") @ mxq(v, 1, "e4m3")
    p = np.tanh(h) * s[:, None, :]
    return mxq(p, 2, "e4m3") @ mxq(u, 1, "e4m3")


def gate_weights(xl, gw):
    t = np.sum(xl[:, None, :] * gw[None, :, :], axis=-1)
    e = np.exp(t - t.max(axis=-1, keepdims=True))
    return e / e.sum(axis=-1, keepdims=True)


def core(x0, xl, v, s, u, gw):
    x0, xl = f64(x0), f64(xl)
    q = expert_outputs(xl, f64(v), f64(s), f64(u))
    a = gate_weights(xl, f64(gw))
    m = np.sum(np.transpose(a)[:, :, None] * q, axis=0)
    return x0 * m + xl


def reference(x0, xl, v, s, u, gw):
    R_out = core(x0, xl, v, s, u, gw)
    words, scales = planes(R_out.T)
    return R_out, words, scales

@@ -1,0 +1,361 @@
+from contextlib import ExitStack
+
+import concourse.mybir as mybir
+from concourse.masks import make_identity
+
+B, D, R, E = 512, 1024, 512, 4
+FLOPS = 2 * E * B * D * R * 2
+
+F32 = mybir.dt.float32
+BF16 = mybir.dt.bfloat16
+U32 = mybir.dt.uint32
+I32 = mybir.dt.int32
+U8 = mybir.dt.uint8
+FP8X4 = mybir.dt.float8_e4m3fn_x4
+ACT = mybir.ActivationFunctionType
+ALU = mybir.AluOpType
+AX = mybir.AxisListType
+
+P = 128
+PACK = 4
+KP = P * PACK
+NT = B // P
+NH = D // KP
+
+
+def tile_crossnetlowrankmixture_x1_kernel(tc, x0, xl, v, s, u, gw, out_0, out_1, out_2):
+    nc = tc.nc
+    with ExitStack() as ctx:
+        keep = ctx.enter_context(tc.tile_pool(name="keep", bufs=1))
+        ring = ctx.enter_context(tc.tile_pool(name="ring", bufs=5))
+        psum = ctx.enter_context(tc.psum_pool(name="psum", bufs=2))
+        ctx.enter_context(tc.manual_schedule())
+
+        def kept(name, shape, dtype):
+            return keep.tile(shape, dtype, name=name, align_bytes=64)
+
+        def bank(tag, shape, dtype):
+            return psum.tile(shape, dtype, name="bank_" + tag, tag=tag, bufs={"turn": 2, "mm": 5, "gate": 1}[tag])
+
+        rows = kept("rows", [P, D], BF16)
+        nc.gpsimd.memset(rows[:].bitcast(F32), 0.0)
+        ident_f = kept("ident_f", [P, P], F32)
+        ident_b = kept("ident_b", [P, P], BF16)
+        make_identity(nc, ident_f[:])
+        make_identity(nc, ident_b[:])
+
+        raw = {}
+        xl_sb, x0_sb = {}, {}
+
+        def load_v(e, g):
+            raw["v", e, g] = kept("v_raw%d%d" % (e, g), [P, PACK, R], BF16)
+            nc.sync.dma_start(out=raw["v", e, g][:], in_=v[e, g * KP:(g + 1) * KP, :].rearrange("(p j) c -> p j c", j=PACK))
+
+        def load_u(e, h):
+            raw["u", e, h] = kept("u_raw%d%d" % (e, h), [P, PACK, KP], BF16)
+            nc.sync.dma_start(out=raw["u", e, h][:], in_=u[e, :, h * KP:(h + 1) * KP].rearrange("(p j) c -> p j c", j=PACK))
+
+        def load_rows(dst, src, name, pair):
+            dst[pair] = kept("%s%d" % (name, pair), [P, 2, D], BF16)
+            nc.sync.dma_start(out=dst[pair][:], in_=src[pair * 2 * P:(pair + 1) * 2 * P, :].rearrange("(t p) d -> p t d", p=P))
+
+        cols = kept("cols", [P, 2 * E, NH, PACK], BF16)
+
+        def load_small():
+            nc.scalar.dma_start(out=rows[0:E, :], in_=gw)
+            nc.scalar.dma_start(out=rows[E:2 * E, 0:R], in_=s)
+            warm = kept("warm", [P, 1], F32)
+            nc.scalar.activation(out=warm[:], in_=ident_f[:, 0:1], func=ACT.Tanh)
+
+        def small_turn():
+            words = rows[:].bitcast(F32)
+            turned = bank("mm", [P, NH * 2, P], F32)
+            for g in range(NH):
+                for w in range(2):
+                    nc.tensor.transpose(turned[:, 2 * g + w, :], words[:, 256 * g + w:256 * (g + 1):2], ident_f[:])
+            nc.scalar.copy(out=cols[:].rearrange("p i g t -> p i (g t)").bitcast(F32), in_=turned[:, :, 0:2 * E].rearrange("p w i -> p i w"))
+
+        load_v(0, 0)
+        load_small()
+        load_rows(xl_sb, xl, "xl", 0)
+        load_v(0, 1)
+        load_rows(xl_sb, xl, "xl", 1)
+        load_v(1, 0)
+        load_v(1, 1)
+        load_v(2, 0)
+        load_v(2, 1)
+        load_u(0, 0)
+        load_v(3, 0)
+        load_v(3, 1)
+        for e in range(1, E):
+            load_u(e, 0)
+        load_u(0, 1)
+        load_rows(x0_sb, x0, "x0", 0)
+        load_rows(x0_sb, x0, "x0", 1)
+        for e in range(1, E):
+            load_u(e, 1)
+
+        grouped, codes, scales = {}, {}, {}
+
+        def quantize(key, src, width):
+            name = "%s%d%d" % key
+            codes[key] = kept("c_" + name, [P, width], U32)
+            scales[key] = kept("s_" + name, [P, width], U8)
+            nc.vector.quantize_mx(out=codes[key][:].bitcast(FP8X4), scales=scales[key][:], in_=src)
+
+        def x_turn(bt):
+            words = xl_sb[bt // 2][:, bt % 2, :].bitcast(F32)
+            turned = bank("mm", [P, NH * 2, P], F32)
+            for g in range(NH):
+                for w in range(2):
+                    nc.tensor.transpose(turned[:, 2 * g + w, :], words[:, 256 * g + w:256 * (g + 1):2], ident_f[:])
+            grouped["x", bt, 0] = kept("xg%d" % bt, [P, NH * P * PACK], BF16)
+            nc.scalar.copy(out=grouped["x", bt, 0][:].bitcast(F32).rearrange("p (g b w) -> p g b w", g=NH, w=2),
+                           in_=turned[:].rearrange("p (g w) b -> p g b w", w=2))
+
+        def quant(kind, i, j):
+            src = grouped[kind, i, j]
+            quantize((kind, i, j), src[:], src.shape[1] // PACK)
+
+        def new_grouped(key):
+            grouped[key] = ring.tile([P, KP * PACK], BF16, name="grouped", tag="grouped", align_bytes=64)
+            return grouped[key]
+
+        def direct(kind, e, i, engine):
+            dst = new_grouped((kind, e, i))
+            copy = nc.vector.tensor_copy if engine == "vector" else nc.scalar.copy
+            if kind == "v":
+                copy(out=dst[:].rearrange("p (t m j) -> p t m j", t=PACK, j=PACK),
+                     in_=raw[kind, e, i][:].rearrange("p j (m t) -> p t m j", t=PACK))
+            else:
+                copy(out=dst[:].rearrange("p (c j) -> p c j", j=PACK), in_=raw[kind, e, i][:].rearrange("p j c -> p c j"))
+
+        def route(kind, e, i):
+            dst = new_grouped((kind, e, i))
+            src = raw[kind, e, i][:].rearrange("p j c -> p c j")
+            for half in range(2):
+                laid = bank("turn", [P, 2 * KP], BF16)
+                for k in range(2):
+                    c0 = (2 * half + k) * P
+                    nc.tensor.matmul(out=laid[:, k * KP:(k + 1) * KP].rearrange("p (c j) -> p c j", j=PACK), lhsT=ident_b[:],
+                                     rhs=src[:, c0:c0 + P, :], start=True, stop=True)
+                if kind == "v":
+                    nc.scalar.copy(out=dst[:].bitcast(F32).rearrange("p (t m w) -> p t m w", t=PACK, w=2)[:, :, half * 64:(half + 1) * 64, :],
+                                   in_=laid[:].bitcast(F32).rearrange("p (m t w) -> p t m w", t=PACK, w=2))
+                else:
+                    nc.scalar.copy(out=dst[:, half * 2 * KP:(half + 1) * 2 * KP].bitcast(F32), in_=laid[:].bitcast(F32))
+
+        tanh_h = {}
+
+        def hidden(e, bt):
+            hb = bank("mm", [P, PACK, P], F32)
+            for t in range(PACK):
+                for g in range(NH):
+                    nc.tensor.matmul_mx(out=hb[:, t, :],
+                                        lhsT=codes["v", e, g][:, t * P:(t + 1) * P].bitcast(FP8X4), lhsT_scale=scales["v", e, g][:, t * P:(t + 1) * P],
+                                        rhs=codes["x", bt, 0][:, g * P:(g + 1) * P].bitcast(FP8X4), rhs_scale=scales["x", bt, 0][:, g * P:(g + 1) * P],
+                                        start=(g == 0), stop=(g == NH - 1))
+            if bt % 2 == 0:
+                tanh_h[e, bt // 2] = ring.tile([P, 2 * P, PACK], F32, name="tanh_h", tag="tanh_h", bufs=4, align_bytes=64)
+            nc.scalar.activation(out=tanh_h[e, bt // 2][:, (bt % 2) * P:(bt % 2 + 1) * P, :], in_=hb[:].rearrange("p t b -> p b t"), func=ACT.Tanh)
+
+        def gain(e, pair):
+            grouped["p", e, pair] = ring.tile([P, 2 * KP], BF16, name="pg", tag="pg", bufs=3, align_bytes=64)
+            nc.vector.tensor_tensor(out=grouped["p", e, pair][:].rearrange("p (b t) -> p b t", t=PACK), in0=tanh_h[e, pair][:],
+                                    in1=cols[:, E + e, 0:1, :].to_broadcast([P, 2 * P, PACK]), op=ALU.mult)
+
+        gate = kept("gate", [P, NT, E], F32)
+        logit = bank("gate", [P, NT, E], F32)
+
+        def logits(bt, step):
+            xg = grouped["x", bt, 0][:].rearrange("p (g b t) -> p g b t", g=NH, t=PACK)
+            for n in (2 * step, 2 * step + 1):
+                g, t = divmod(n, PACK)
+                nc.tensor.matmul(out=logit[:, bt, :], lhsT=xg[:, g, :, t], rhs=cols[:, 0:E, g, t], start=(n == 0), stop=(n == NH * PACK - 1))
+
+        top = kept("top", [P, NT], F32)
+        shifted = kept("shifted", [P, NT, E], F32)
+        total = kept("total", [P, NT], F32)
+        inv = kept("inv", [P, NT], F32)
+
+        def soft(step):
+            if step == 0:
+                nc.vector.tensor_reduce(out=top[:], in_=logit[:], axis=AX.X, op=ALU.max)
+            elif step == 1:
+                nc.vector.tensor_tensor(out=shifted[:], in0=logit[:], in1=top[:].unsqueeze(2).to_broadcast([P, NT, E]), op=ALU.subtract)
+                nc.scalar.activation(out=shifted[:], in_=shifted[:], func=ACT.Exp)
+            elif step == 2:
+                nc.vector.tensor_reduce(out=total[:], in_=shifted[:], axis=AX.X, op=ALU.add)
+            elif step == 3:
+                nc.vector.reciprocal(out=inv[:], in_=total[:])
+            else:
+                nc.vector.tensor_tensor(out=gate[:], in0=shifted[:], in1=inv[:].unsqueeze(2).to_broadcast([P, NT, E]), op=ALU.mult)
+
+        acc = {}
+        for h in range(NH):
+            for pair in range(2):
+                acc[h, pair] = kept("acc%d%d" % (h, pair), [P, 2, KP], F32)
+
+        def mix(e, h, bt):
+            qb = bank("mm", [P, KP], F32)
+            span = slice((bt % 2) * P, (bt % 2 + 1) * P)
+            nc.tensor.matmul_mx(out=qb[:], lhsT=codes["p", e, bt // 2][:, span].bitcast(FP8X4), lhsT_scale=scales["p", e, bt // 2][:, span],
+                                rhs=codes["u", e, h][:].bitcast(FP8X4), rhs_scale=scales["u", e, h][:], start=True, stop=True)
+            dst = acc[h, bt // 2][:, bt % 2, :]
+            if e == 0:
+                nc.scalar.activation(out=dst, in_=qb[:], func=ACT.Copy, scale=gate[:, bt, 0:1])
+            else:
+                nc.vector.scalar_tensor_tensor(out=dst, in0=qb[:], scalar=gate[:, bt, e:e + 1], in1=dst, op0=ALU.mult, op1=ALU.add)
+
+        def times_x0(h, bts):
+            dst = acc[h, bts[0] // 2][:, bts[0] % 2:bts[-1] % 2 + 1, :]
+            nc.vector.tensor_tensor(out=dst, in0=dst, in1=x0_sb[bts[0] // 2][:, bts[0] % 2:bts[-1] % 2 + 1, h * KP:(h + 1) * KP], op=ALU.mult)
+
+        def plus_xl(h, bt, engine):
+            dst = acc[h, bt // 2][:, bt % 2, :]
+            engine.tensor_tensor(out=dst, in0=dst, in1=xl_sb[bt // 2][:, bt % 2, h * KP:(h + 1) * KP], op=ALU.add)
+            nc.sync.dma_start(out=out_0[bt * P:(bt + 1) * P, h * KP:(h + 1) * KP], in_=dst)
+
+        rounded_words = {}
+
+        def out_round(h, bts):
+            n = len(bts)
+            rounded = ring.tile([P, n, 2, P, 2], BF16, name="rounded", tag="rounded", bufs=2, align_bytes=64)
+            src = acc[h, bts[0] // 2][:, bts[0] % 2:bts[-1] % 2 + 1, :]
+            nc.scalar.copy(out=rounded[:], in_=src.rearrange("b n (p w i) -> b n w p i", w=2, i=2))
+            rounded_words[h, bts] = rounded[:].rearrange("b n w p i -> b (n w p i)").bitcast(F32)
+
+        def out_turn(h, bts):
+            n = len(bts)
+            words = rounded_words[h, bts]
+            turned = bank("turn", [P, n, 2, P], F32)
+            for i in range(n):
+                for w in range(2):
+                    nc.tensor.transpose(turned[:, i, w, :], words[:, (2 * i + w) * P:(2 * i + w + 1) * P], ident_f[:])
+            grouped["o", h, bts[0]] = ring.tile([P, n * KP], BF16, name="og", tag="og", bufs=3, align_bytes=64)
+            nc.scalar.copy(out=grouped["o", h, bts[0]][:].bitcast(F32).rearrange("p (n b w) -> p n b w", n=n, w=2),
+                           in_=turned[:].rearrange("p n w b -> p n b w"))
+
+        out_scales = [kept("out_scales%d" % h, [P, B], U8) for h in range(NH)]
+
+        def out_quant(h, bts):
+            span = slice(bts[0] * P, (bts[-1] + 1) * P)
+            words = kept("out_words%d%d" % (h, bts[0]), [P, len(bts) * P], I32)
+            nc.vector.quantize_mx(out=words[:].bitcast(FP8X4), scales=out_scales[h][:, span],
+                                  in_=grouped["o", h, bts[0]][:])
+            nc.sync.dma_start(out=out_1[h].rearrange("p m t -> p (m t)").bitcast(I32)[:, span], in_=words[:])
+            if bts[-1] == NT - 1:
+                for q in range(4):
+                    queue = nc.scalar if (h == NH - 1 and q % 2) else nc.sync
+                    queue.dma_start(out=out_2[h, 4 * q:4 * q + 4, :].bitcast(I32), in_=out_scales[h][32 * q:32 * q + 4, :].bitcast(I32))
+
+        ADD = nc.gpsimd
+        units = [(h, (2 * pair, 2 * pair + 1)) for h in range(NH) for pair in range(2)]
+        direct("v", 0, 0, "vector")
+        x_turn(0)
+        x_turn(1)
+        quant("v", 0, 0)
+        direct("v", 0, 1, "vector")
+        quant("x", 0, 0)
+        quant("v", 0, 1)
+        quant("x", 1, 0)
+        small_turn()
+        direct("v", 1, 0, "vector")
+        hidden(0, 0)
+        hidden(0, 1)
+        x_turn(2)
+        x_turn(3)
+        quant("v", 1, 0)
+        route("v", 1, 1)
+        direct("v", 2, 0, "vector")
+        quant("x", 2, 0)
+        quant("x", 3, 0)
+        hidden(0, 2)
+        hidden(0, 3)
+        for e in range(E - 1):
+            if e < 2:
+                route("v", e + 2, 1)
+            else:
+                route("u", 2, 0)
+            if e == 0:
+                gain(e, 0)
+            quant("v", e + 1, 1)
+            if e < 2:
+                direct("u", e, 0, "scalar")
+                quant("v", e + 2, 0)
+            if e > 0:
+                gain(e, 0)
+            if e == 0:
+                direct("v", 3, 0, "vector")
+            if e == 2:
+                soft(0)
+            if e > 0:
+                quant("u", e - 1, 0)
+            if e == 2:
+                soft(1)
+            gain(e, 1)
+            for bt in range(NT):
+                hidden(e + 1, bt)
+                if e < 2:
+                    logits(2 * e + bt // 2, 2 * (bt % 2))
+                    logits(2 * e + bt // 2, 2 * (bt % 2) + 1)
+            if e == 2:
+                soft(2)
+            quant("p", e, 0)
+            if e == 2:
+                soft(3)
+            quant("p", e, 1)
+        soft(4)
+        quant("u", 2, 0)
+        for bt in (0, 1):
+            mix(0, 0, bt)
+        route("u", 3, 0)
+        gain(3, 0)
+        for bt in (0, 1):
+            mix(1, 0, bt)
+        direct("u", 0, 1, "scalar")
+        quant("p", 3, 0)
+        quant("u", 3, 0)
+        for bt in (2, 3):
+            mix(0, 0, bt)
+        direct("u", 1, 1, "scalar")
+        gain(3, 1)
+        for bt in (0, 1):
+            mix(2, 0, bt)
+        quant("p", 3, 1)
+
+        for k, (h, bts) in enumerate(units):
+            for e in range(1 if k else 3, E):
+                for bt in bts:
+                    mix(e, h, bt)
+                if e == 2 and k >= 2:
+                    out_turn(*units[k - 2])
+            if k == 0:
+                direct("u", 2, 1, "scalar")
+                route("u", 3, 1)
+            if k < 2:
+                quant("u", 2 * k, 1)
+                quant("u", 2 * k + 1, 1)
+            if 0 < k < len(units) - 1:
+                for bt in units[k + 1][1]:
+                    mix(0, units[k + 1][0], bt)
+            if k >= 1:
+                out_round(*units[k - 1])
+            if k >= 2:
+                out_quant(*units[k - 2])
+            if k + 1 < len(units):
+                times_x0(h, bts)
+                for bt in bts:
+                    plus_xl(h, bt, ADD)
+            else:
+                out_turn(*units[k - 1])
+                for bt in bts:
+                    times_x0(h, (bt,))
+                for bt in bts:
+                    plus_xl(h, bt, nc.vector)
+                    out_round(h, (bt,))
+                for bt in bts:
+                    out_turn(h, (bt,))
+                out_quant(*units[k - 1])
+                for bt in bts:
+                    out_quant(h, (bt,))

@@ -21,6 +21,8 @@ PACK = 4
 KP = P * PACK
 NT = B // P
 NH = D // KP
+RUN = 8
+NQ = P // RUN
 
 
 def tile_crossnetlowrankmixture_x1_kernel(tc, x0, xl, v, s, u, gw, out_0, out_1, out_2):
@@ -34,8 +36,12 @@ def tile_crossnetlowrankmixture_x1_kernel(tc, x0, xl, v, s, u, gw, out_0, out_1,
         def kept(name, shape, dtype):
             return keep.tile(shape, dtype, name=name, align_bytes=64)
 
-        def bank(tag, shape, dtype):
-            return psum.tile(shape, dtype, name="bank_" + tag, tag=tag, bufs={"turn": 2, "mm": 5, "gate": 1}[tag])
+        rotation = {"turn": ["b0", "b1"], "mm": ["b2", "b3", "b4", "b5"], "gate": ["b6"], "gain": ["b7"]}
+
+        def bank(role, shape, dtype):
+            tag = rotation[role][0]
+            rotation[role] = rotation[role][1:] + [tag]
+            return psum.tile(shape, dtype, name=tag, tag=tag, bufs=1)
 
         rows = kept("rows", [P, D], BF16)
         nc.gpsimd.memset(rows[:].bitcast(F32), 0.0)
@@ -48,18 +54,23 @@ def tile_crossnetlowrankmixture_x1_kernel(tc, x0, xl, v, s, u, gw, out_0, out_1,
         xl_sb, x0_sb = {}, {}
 
         def load_v(e, g):
-            raw["v", e, g] = kept("v_raw%d%d" % (e, g), [P, PACK, R], BF16)
-            nc.sync.dma_start(out=raw["v", e, g][:], in_=v[e, g * KP:(g + 1) * KP, :].rearrange("(p j) c -> p j c", j=PACK))
+            tile = kept("v_raw%d%d" % (e, g), [P, PACK, R], BF16)
+            raw["v", e, g] = tile[:]
+            nc.sync.dma_start(out=tile[:], in_=v[e, g * KP:(g + 1) * KP, :].rearrange("(p j) c -> p j c", j=PACK))
 
-        def load_u(e, h):
-            raw["u", e, h] = kept("u_raw%d%d" % (e, h), [P, PACK, KP], BF16)
-            nc.sync.dma_start(out=raw["u", e, h][:], in_=u[e, :, h * KP:(h + 1) * KP].rearrange("(p j) c -> p j c", j=PACK))
+        def load_u(e):
+            whole = kept("u_raw%d" % e, [P, PACK, D], BF16)
+            rows_in_runs = u[e].rearrange("(q t r) d -> t q r d", t=PACK, r=RUN)
+            for t in range(PACK):
+                nc.sync.dma_start(out=whole[:, t, :], in_=rows_in_runs[t])
+            for h in range(NH):
+                raw["u", e, h] = whole[:, :, h * KP:(h + 1) * KP]
 
         def load_rows(dst, src, name, pair):
             dst[pair] = kept("%s%d" % (name, pair), [P, 2, D], BF16)
             nc.sync.dma_start(out=dst[pair][:], in_=src[pair * 2 * P:(pair + 1) * 2 * P, :].rearrange("(t p) d -> p t d", p=P))
 
-        cols = kept("cols", [P, 2 * E, NH, PACK], BF16)
+        cols = kept("cols", [P, E, NH, PACK], BF16)
 
         def load_small():
             nc.scalar.dma_start(out=rows[0:E, :], in_=gw)
@@ -67,13 +78,24 @@ def tile_crossnetlowrankmixture_x1_kernel(tc, x0, xl, v, s, u, gw, out_0, out_1,
             warm = kept("warm", [P, 1], F32)
             nc.scalar.activation(out=warm[:], in_=ident_f[:, 0:1], func=ACT.Tanh)
 
-        def small_turn():
+        gains = bank("gain", [P, PACK, P], F32)
+
+        def gate_turn():
             words = rows[:].bitcast(F32)
             turned = bank("mm", [P, NH * 2, P], F32)
             for g in range(NH):
                 for w in range(2):
                     nc.tensor.transpose(turned[:, 2 * g + w, :], words[:, 256 * g + w:256 * (g + 1):2], ident_f[:])
-            nc.scalar.copy(out=cols[:].rearrange("p i g t -> p i (g t)").bitcast(F32), in_=turned[:, :, 0:2 * E].rearrange("p w i -> p i w"))
+            nc.scalar.copy(out=cols[:].rearrange("p i g t -> p i (g t)").bitcast(F32), in_=turned[:, :, 0:E].rearrange("p w i -> p i w"))
+
+        s_sorted = kept("s_sorted", [P, PACK, P], F32)
+
+        def gain_sort():
+            nc.scalar.copy(out=s_sorted[:].rearrange("i t (q r) -> i t q r", r=RUN), in_=rows[:, 0:R].rearrange("i (q t r) -> i t q r", t=PACK, r=RUN))
+
+        def gain_turn():
+            for t in range(PACK):
+                nc.tensor.transpose(gains[:, t, :], s_sorted[:, t, :], ident_f[:])
 
         load_v(0, 0)
         load_small()
@@ -84,24 +106,36 @@ def tile_crossnetlowrankmixture_x1_kernel(tc, x0, xl, v, s, u, gw, out_0, out_1,
         load_v(1, 1)
         load_v(2, 0)
         load_v(2, 1)
-        load_u(0, 0)
+        load_u(0)
         load_v(3, 0)
         load_v(3, 1)
         for e in range(1, E):
-            load_u(e, 0)
-        load_u(0, 1)
+            load_u(e)
         load_rows(x0_sb, x0, "x0", 0)
         load_rows(x0_sb, x0, "x0", 1)
-        for e in range(1, E):
-            load_u(e, 1)
 
         grouped, codes, scales = {}, {}, {}
 
-        def quantize(key, src, width):
-            name = "%s%d%d" % key
-            codes[key] = kept("c_" + name, [P, width], U32)
-            scales[key] = kept("s_" + name, [P, width], U8)
-            nc.vector.quantize_mx(out=codes[key][:].bitcast(FP8X4), scales=scales[key][:], in_=src)
+        def quant(*keys):
+            name = "%s%d%d" % keys[0]
+            whole, first = home[keys[0]]
+            width = grouped[keys[0]].shape[1] // PACK
+            code_tile = kept("c_" + name, [P, len(keys) * width], U32)
+            scale_tile = kept("s_" + name, [P, len(keys) * width], U8)
+            nc.vector.quantize_mx(out=code_tile[:].bitcast(FP8X4), scales=scale_tile[:],
+                                  in_=whole[:, first:first + len(keys) * width * PACK])
+            for n, key in enumerate(keys):
+                assert home[key] == (whole, first + n * width * PACK)
+                codes[key] = code_tile[:, n * width:(n + 1) * width]
+                scales[key] = scale_tile[:, n * width:(n + 1) * width]
+
+        home = {}
+
+        def room(tag, bufs, width, *keys):
+            whole = ring.tile([P, len(keys) * width], BF16, name=tag, tag=tag, bufs=bufs, align_bytes=64)
+            for n, key in enumerate(keys):
+                home[key] = (whole, n * width)
+                grouped[key] = whole[:, n * width:(n + 1) * width]
 
         def x_turn(bt):
             words = xl_sb[bt // 2][:, bt % 2, :].bitcast(F32)
@@ -109,30 +143,31 @@ def tile_crossnetlowrankmixture_x1_kernel(tc, x0, xl, v, s, u, gw, out_0, out_1,
             for g in range(NH):
                 for w in range(2):
                     nc.tensor.transpose(turned[:, 2 * g + w, :], words[:, 256 * g + w:256 * (g + 1):2], ident_f[:])
-            grouped["x", bt, 0] = kept("xg%d" % bt, [P, NH * P * PACK], BF16)
+            room("xg", NT, NH * P * PACK, ("x", bt, 0))
             nc.scalar.copy(out=grouped["x", bt, 0][:].bitcast(F32).rearrange("p (g b w) -> p g b w", g=NH, w=2),
                            in_=turned[:].rearrange("p (g w) b -> p g b w", w=2))
 
-        def quant(kind, i, j):
-            src = grouped[kind, i, j]
-            quantize((kind, i, j), src[:], src.shape[1] // PACK)
+        def pool_copy(out, in_):
+            nc.gpsimd.tensor_scalar(out=out, in0=in_, scalar1=1.0, scalar2=0.0, op0=ALU.mult, op1=ALU.add)
 
-        def new_grouped(key):
-            grouped[key] = ring.tile([P, KP * PACK], BF16, name="grouped", tag="grouped", align_bytes=64)
-            return grouped[key]
-
-        def direct(kind, e, i, engine):
-            dst = new_grouped((kind, e, i))
-            copy = nc.vector.tensor_copy if engine == "vector" else nc.scalar.copy
-            if kind == "v":
-                copy(out=dst[:].rearrange("p (t m j) -> p t m j", t=PACK, j=PACK),
-                     in_=raw[kind, e, i][:].rearrange("p j (m t) -> p t m j", t=PACK))
+        def direct(kind, e, i, engine, lo=0, hi=NQ):
+            if (kind, e, i) not in grouped:
+                room("grouped", 5, KP * PACK, (kind, e, i))
+            dst = grouped[kind, e, i]
+            copy = {"vector": nc.vector.tensor_copy, "scalar": nc.scalar.copy, "gpsimd": pool_copy}[engine]
+            if engine == "gpsimd" and kind == "u":
+                copy(out=dst.rearrange("p (c j) -> p c j", j=PACK)[:, lo * 32:hi * 32], in_=raw[kind, e, i].rearrange("p j c -> p c j")[:, lo * 32:hi * 32])
+            elif kind == "v":
+                copy(out=dst.rearrange("p (t q r j) -> p q t r j", t=PACK, r=RUN, j=PACK)[:, lo:hi],
+                     in_=raw[kind, e, i].rearrange("p j (q t r) -> p q t r j", t=PACK, r=RUN)[:, lo:hi])
             else:
-                copy(out=dst[:].rearrange("p (c j) -> p c j", j=PACK), in_=raw[kind, e, i][:].rearrange("p j c -> p c j"))
+                copy(out=dst.rearrange("p (c i j) -> p c j i", i=4, j=PACK)[:, lo * 8:hi * 8], in_=raw[kind, e, i].rearrange("p j (c i) -> p c j i", i=4)[:, lo * 8:hi * 8])
 
         def route(kind, e, i):
-            dst = new_grouped((kind, e, i))
-            src = raw[kind, e, i][:].rearrange("p j c -> p c j")
+            if (kind, e, i) not in grouped:
+                room("grouped", 5, KP * PACK, (kind, e, i))
+            dst = grouped[kind, e, i]
+            src = raw[kind, e, i].rearrange("p j c -> p c j")
             for half in range(2):
                 laid = bank("turn", [P, 2 * KP], BF16)
                 for k in range(2):
@@ -140,8 +175,8 @@ def tile_crossnetlowrankmixture_x1_kernel(tc, x0, xl, v, s, u, gw, out_0, out_1,
                     nc.tensor.matmul(out=laid[:, k * KP:(k + 1) * KP].rearrange("p (c j) -> p c j", j=PACK), lhsT=ident_b[:],
                                      rhs=src[:, c0:c0 + P, :], start=True, stop=True)
                 if kind == "v":
-                    nc.scalar.copy(out=dst[:].bitcast(F32).rearrange("p (t m w) -> p t m w", t=PACK, w=2)[:, :, half * 64:(half + 1) * 64, :],
-                                   in_=laid[:].bitcast(F32).rearrange("p (m t w) -> p t m w", t=PACK, w=2))
+                    nc.scalar.copy(out=dst.bitcast(F32).rearrange("p (t q w) -> p q t w", t=PACK, q=NQ)[:, half * RUN:(half + 1) * RUN],
+                                   in_=laid[:].bitcast(F32).rearrange("p (q t w) -> p q t w", t=PACK, q=RUN))
                 else:
                     nc.scalar.copy(out=dst[:, half * 2 * KP:(half + 1) * 2 * KP].bitcast(F32), in_=laid[:].bitcast(F32))
 
@@ -155,14 +190,18 @@ def tile_crossnetlowrankmixture_x1_kernel(tc, x0, xl, v, s, u, gw, out_0, out_1,
                                         lhsT=codes["v", e, g][:, t * P:(t + 1) * P].bitcast(FP8X4), lhsT_scale=scales["v", e, g][:, t * P:(t + 1) * P],
                                         rhs=codes["x", bt, 0][:, g * P:(g + 1) * P].bitcast(FP8X4), rhs_scale=scales["x", bt, 0][:, g * P:(g + 1) * P],
                                         start=(g == 0), stop=(g == NH - 1))
-            if bt % 2 == 0:
-                tanh_h[e, bt // 2] = ring.tile([P, 2 * P, PACK], F32, name="tanh_h", tag="tanh_h", bufs=4, align_bytes=64)
-            nc.scalar.activation(out=tanh_h[e, bt // 2][:, (bt % 2) * P:(bt % 2 + 1) * P, :], in_=hb[:].rearrange("p t b -> p b t"), func=ACT.Tanh)
+            if bt == 0:
+                tanh_h[e] = ring.tile([P, B, PACK], F32, name="tanh_h", tag="tanh_h", bufs=2, align_bytes=64)
+            nc.scalar.activation(out=tanh_h[e][:, bt * P:(bt + 1) * P, :], in_=hb[:].rearrange("p t b -> p b t"), func=ACT.Tanh)
 
-        def gain(e, pair):
-            grouped["p", e, pair] = ring.tile([P, 2 * KP], BF16, name="pg", tag="pg", bufs=3, align_bytes=64)
-            nc.vector.tensor_tensor(out=grouped["p", e, pair][:].rearrange("p (b t) -> p b t", t=PACK), in0=tanh_h[e, pair][:],
-                                    in1=cols[:, E + e, 0:1, :].to_broadcast([P, 2 * P, PACK]), op=ALU.mult)
+        def gain(e, *pairs):
+            if pairs[0] == 0:
+                room("pg", 2, 2 * KP, ("p", e, 0), ("p", e, 1))
+            whole, first = home["p", e, pairs[0]]
+            n = 2 * P * len(pairs)
+            nc.vector.tensor_tensor(out=whole[:, first:first + n * PACK].rearrange("p (b t) -> p b t", t=PACK),
+                                    in0=tanh_h[e][:, pairs[0] * 2 * P:pairs[0] * 2 * P + n, :],
+                                    in1=gains[:, :, E + e:E + e + 1].rearrange("p t o -> p o t").to_broadcast([P, n, PACK]), op=ALU.mult)
 
         gate = kept("gate", [P, NT, E], F32)
         logit = bank("gate", [P, NT, E], F32)
@@ -171,7 +210,7 @@ def tile_crossnetlowrankmixture_x1_kernel(tc, x0, xl, v, s, u, gw, out_0, out_1,
             xg = grouped["x", bt, 0][:].rearrange("p (g b t) -> p g b t", g=NH, t=PACK)
             for n in (2 * step, 2 * step + 1):
                 g, t = divmod(n, PACK)
-                nc.tensor.matmul(out=logit[:, bt, :], lhsT=xg[:, g, :, t], rhs=cols[:, 0:E, g, t], start=(n == 0), stop=(n == NH * PACK - 1))
+                nc.tensor.matmul(out=logit[:, bt, :], lhsT=xg[:, g, :, t], rhs=cols[:, :, g, t], start=(n == 0), stop=(n == NH * PACK - 1))
 
         top = kept("top", [P, NT], F32)
         shifted = kept("shifted", [P, NT, E], F32)
@@ -207,9 +246,9 @@ def tile_crossnetlowrankmixture_x1_kernel(tc, x0, xl, v, s, u, gw, out_0, out_1,
             else:
                 nc.vector.scalar_tensor_tensor(out=dst, in0=qb[:], scalar=gate[:, bt, e:e + 1], in1=dst, op0=ALU.mult, op1=ALU.add)
 
-        def times_x0(h, bts):
+        def times_x0(h, bts, engine=nc.vector):
             dst = acc[h, bts[0] // 2][:, bts[0] % 2:bts[-1] % 2 + 1, :]
-            nc.vector.tensor_tensor(out=dst, in0=dst, in1=x0_sb[bts[0] // 2][:, bts[0] % 2:bts[-1] % 2 + 1, h * KP:(h + 1) * KP], op=ALU.mult)
+            engine.tensor_tensor(out=dst, in0=dst, in1=x0_sb[bts[0] // 2][:, bts[0] % 2:bts[-1] % 2 + 1, h * KP:(h + 1) * KP], op=ALU.mult)
 
         def plus_xl(h, bt, engine):
             dst = acc[h, bt // 2][:, bt % 2, :]
@@ -217,6 +256,12 @@ def tile_crossnetlowrankmixture_x1_kernel(tc, x0, xl, v, s, u, gw, out_0, out_1,
             nc.sync.dma_start(out=out_0[bt * P:(bt + 1) * P, h * KP:(h + 1) * KP], in_=dst)
 
         rounded_words = {}
+
+        def plus_xl_rounded(h, bt):
+            rounded = ring.tile([P, 1, 2, P, 2], BF16, name="rounded", tag="rounded", bufs=2, align_bytes=64)
+            nc.vector.tensor_tensor(out=rounded[:, 0], in0=acc[h, bt // 2][:, bt % 2, :].rearrange("b (p w i) -> b w p i", w=2, i=2),
+                                    in1=xl_sb[bt // 2][:, bt % 2, h * KP:(h + 1) * KP].rearrange("b (p w i) -> b w p i", w=2, i=2), op=ALU.add)
+            rounded_words[h, (bt,)] = rounded[:].rearrange("b n w p i -> b (n w p i)").bitcast(F32)
 
         def out_round(h, bts):
             n = len(bts)
@@ -249,93 +294,89 @@ def tile_crossnetlowrankmixture_x1_kernel(tc, x0, xl, v, s, u, gw, out_0, out_1,
                     queue = nc.scalar if (h == NH - 1 and q % 2) else nc.sync
                     queue.dma_start(out=out_2[h, 4 * q:4 * q + 4, :].bitcast(I32), in_=out_scales[h][32 * q:32 * q + 4, :].bitcast(I32))
 
+        def handover(key):
+            room("handover", 1, KP * PACK, key)
+
         ADD = nc.gpsimd
         units = [(h, (2 * pair, 2 * pair + 1)) for h in range(NH) for pair in range(2)]
         direct("v", 0, 0, "vector")
+        gain_sort()
         x_turn(0)
         x_turn(1)
-        quant("v", 0, 0)
+        quant(("v", 0, 0))
         direct("v", 0, 1, "vector")
-        quant("x", 0, 0)
-        quant("v", 0, 1)
-        quant("x", 1, 0)
-        small_turn()
+        quant(("x", 0, 0))
+        quant(("v", 0, 1))
+        quant(("x", 1, 0))
+        gain_turn()
         direct("v", 1, 0, "vector")
         hidden(0, 0)
         hidden(0, 1)
         x_turn(2)
         x_turn(3)
-        quant("v", 1, 0)
+        quant(("v", 1, 0))
         route("v", 1, 1)
+        handover(("v", 2, 0))
         direct("v", 2, 0, "vector")
-        quant("x", 2, 0)
-        quant("x", 3, 0)
+        quant(("x", 2, 0))
+        quant(("x", 3, 0))
         hidden(0, 2)
         hidden(0, 3)
-        for e in range(E - 1):
-            if e < 2:
-                route("v", e + 2, 1)
-            else:
-                route("u", 2, 0)
-            if e == 0:
-                gain(e, 0)
-            quant("v", e + 1, 1)
-            if e < 2:
-                direct("u", e, 0, "scalar")
-                quant("v", e + 2, 0)
-            if e > 0:
-                gain(e, 0)
-            if e == 0:
-                direct("v", 3, 0, "vector")
+        gate_turn()
+        by_pool = [("v", 2, 1), ("v", 3, 1), ("u", 2, 0), ("u", 3, 0), ("u", 0, 1)]
+        by_scalar = [("v", 3, 0), ("u", 0, 0), ("u", 1, 0)]
+        quant(("v", 1, 1))
+        quant(("v", 2, 0))
+        for e in range(E):
+            handover(by_pool[e])
+            direct(*by_pool[e], "gpsimd")
+            gain(e, 0)
             if e == 2:
                 soft(0)
-            if e > 0:
-                quant("u", e - 1, 0)
+            gain(e, 1)
             if e == 2:
                 soft(1)
-            gain(e, 1)
-            for bt in range(NT):
-                hidden(e + 1, bt)
-                if e < 2:
-                    logits(2 * e + bt // 2, 2 * (bt % 2))
-                    logits(2 * e + bt // 2, 2 * (bt % 2) + 1)
+            if e + 1 < E:
+                for bt in range(NT):
+                    hidden(e + 1, bt)
+                    if e < 2:
+                        logits(2 * e + bt // 2, 2 * (bt % 2))
+                        logits(2 * e + bt // 2, 2 * (bt % 2) + 1)
+                direct(*by_scalar[e], "scalar")
+            if e == 3:
+                rotation["mm"] = rotation["mm"] + rotation["gate"] + rotation["gain"]
+                for bt in range(NT):
+                    mix(0, 0, bt)
+                route("u", 1, 1)
+            quant(("p", e, 0))
             if e == 2:
                 soft(2)
-            quant("p", e, 0)
+            quant(("p", e, 1))
             if e == 2:
                 soft(3)
-            quant("p", e, 1)
-        soft(4)
-        quant("u", 2, 0)
-        for bt in (0, 1):
-            mix(0, 0, bt)
-        route("u", 3, 0)
-        gain(3, 0)
-        for bt in (0, 1):
-            mix(1, 0, bt)
-        direct("u", 0, 1, "scalar")
-        quant("p", 3, 0)
-        quant("u", 3, 0)
-        for bt in (2, 3):
-            mix(0, 0, bt)
-        direct("u", 1, 1, "scalar")
-        gain(3, 1)
-        for bt in (0, 1):
-            mix(2, 0, bt)
-        quant("p", 3, 1)
+            if e > 0:
+                quant(by_scalar[e - 1])
+            if e == 2:
+                soft(4)
+            quant(by_pool[e])
+        handover(by_pool[E])
+        direct(*by_pool[E], "gpsimd")
 
         for k, (h, bts) in enumerate(units):
-            for e in range(1 if k else 3, E):
+            for e in range(1, E):
                 for bt in bts:
                     mix(e, h, bt)
+                if e == 2 and k == 1:
+                    route("u", 3, 1)
                 if e == 2 and k >= 2:
                     out_turn(*units[k - 2])
             if k == 0:
-                direct("u", 2, 1, "scalar")
-                route("u", 3, 1)
-            if k < 2:
-                quant("u", 2 * k, 1)
-                quant("u", 2 * k + 1, 1)
+                quant(("u", 1, 1))
+                route("u", 2, 1)
+            if k == 1:
+                quant(("u", 0, 1))
+                quant(("u", 2, 1))
+                quant(("u", 3, 1))
             if 0 < k < len(units) - 1:
                 for bt in units[k + 1][1]:
                     mix(0, units[k + 1][0], bt)

@@ -23,35 +23,36 @@ NT = B // P
 NH = D // KP
 RUN = 8
 NQ = P // RUN
+NEAR = 4
+LOGITS_PER_TILE = 4
 
 
 def tile_crossnetlowrankmixture_x1_kernel(tc, x0, xl, v, s, u, gw, out_0, out_1, out_2):
     nc = tc.nc
     with ExitStack() as ctx:
         keep = ctx.enter_context(tc.tile_pool(name="keep", bufs=1))
-        ring = ctx.enter_context(tc.tile_pool(name="ring", bufs=5))
-        psum = ctx.enter_context(tc.psum_pool(name="psum", bufs=2))
+        ring = ctx.enter_context(tc.tile_pool(name="ring", bufs=2))
+        psum = ctx.enter_context(tc.psum_pool(name="psum", bufs=1))
         ctx.enter_context(tc.manual_schedule())
 
         def kept(name, shape, dtype):
             return keep.tile(shape, dtype, name=name, align_bytes=64)
 
-        rotation = {"turn": ["b0", "b1"], "mm": ["b2", "b3", "b4", "b5"], "gate": ["b6"], "gain": ["b7"]}
+        rotation = {"turn": ["b0", "b1"], "product": ["b2", "b3", "b4", "b5"], "gate": ["b6"], "gain": ["b7"]}
 
         def bank(role, shape, dtype):
             tag = rotation[role][0]
             rotation[role] = rotation[role][1:] + [tag]
-            return psum.tile(shape, dtype, name=tag, tag=tag, bufs=1)
+            return psum.tile(shape, dtype, name=tag, tag=tag)
 
-        rows = kept("rows", [P, D], BF16)
-        nc.gpsimd.memset(rows[:].bitcast(F32), 0.0)
+        small_rows = kept("small_rows", [P, D], BF16)
+        nc.gpsimd.memset(small_rows[:].bitcast(F32), 0.0)
         ident_f = kept("ident_f", [P, P], F32)
         ident_b = kept("ident_b", [P, P], BF16)
         make_identity(nc, ident_f[:])
         make_identity(nc, ident_b[:])
 
-        raw = {}
-        xl_sb, x0_sb = {}, {}
+        raw, xl_sb, x0_sb = {}, {}, {}
 
         def load_v(e, g):
             tile = kept("v_raw%d%d" % (e, g), [P, PACK, R], BF16)
@@ -59,131 +60,115 @@ def tile_crossnetlowrankmixture_x1_kernel(tc, x0, xl, v, s, u, gw, out_0, out_1,
             nc.sync.dma_start(out=tile[:], in_=v[e, g * KP:(g + 1) * KP, :].rearrange("(p j) c -> p j c", j=PACK))
 
         def load_u(e):
-            whole = kept("u_raw%d" % e, [P, PACK, D], BF16)
-            rows_in_runs = u[e].rearrange("(q t r) d -> t q r d", t=PACK, r=RUN)
+            tile = kept("u_raw%d" % e, [P, PACK, D], BF16)
+            rows_by_value = u[e].rearrange("(q t i) d -> t q i d", t=PACK, i=RUN)
             for t in range(PACK):
-                nc.sync.dma_start(out=whole[:, t, :], in_=rows_in_runs[t])
+                nc.sync.dma_start(out=tile[:, t, :], in_=rows_by_value[t])
             for h in range(NH):
-                raw["u", e, h] = whole[:, :, h * KP:(h + 1) * KP]
+                raw["u", e, h] = tile[:, :, h * KP:(h + 1) * KP]
 
-        def load_rows(dst, src, name, pair):
+        def load_tokens(dst, src, name, pair):
             dst[pair] = kept("%s%d" % (name, pair), [P, 2, D], BF16)
-            nc.sync.dma_start(out=dst[pair][:], in_=src[pair * 2 * P:(pair + 1) * 2 * P, :].rearrange("(t p) d -> p t d", p=P))
-
-        cols = kept("cols", [P, E, NH, PACK], BF16)
-
-        def load_small():
-            nc.scalar.dma_start(out=rows[0:E, :], in_=gw)
-            nc.scalar.dma_start(out=rows[E:2 * E, 0:R], in_=s)
-            warm = kept("warm", [P, 1], F32)
-            nc.scalar.activation(out=warm[:], in_=ident_f[:, 0:1], func=ACT.Tanh)
-
-        gains = bank("gain", [P, PACK, P], F32)
-
-        def gate_turn():
-            words = rows[:].bitcast(F32)
-            turned = bank("mm", [P, NH * 2, P], F32)
-            for g in range(NH):
-                for w in range(2):
-                    nc.tensor.transpose(turned[:, 2 * g + w, :], words[:, 256 * g + w:256 * (g + 1):2], ident_f[:])
-            nc.scalar.copy(out=cols[:].rearrange("p i g t -> p i (g t)").bitcast(F32), in_=turned[:, :, 0:E].rearrange("p w i -> p i w"))
-
-        s_sorted = kept("s_sorted", [P, PACK, P], F32)
-
-        def gain_sort():
-            nc.scalar.copy(out=s_sorted[:].rearrange("i t (q r) -> i t q r", r=RUN), in_=rows[:, 0:R].rearrange("i (q t r) -> i t q r", t=PACK, r=RUN))
-
-        def gain_turn():
-            for t in range(PACK):
-                nc.tensor.transpose(gains[:, t, :], s_sorted[:, t, :], ident_f[:])
+            nc.sync.dma_start(out=dst[pair][:], in_=src[pair * 2 * P:(pair + 1) * 2 * P, :].rearrange("(n p) d -> p n d", p=P))
 
         load_v(0, 0)
-        load_small()
-        load_rows(xl_sb, xl, "xl", 0)
+        nc.sync.dma_start(out=small_rows[0:E, :], in_=gw)
+        nc.sync.dma_start(out=small_rows[E:2 * E, 0:R], in_=s)
+        table_warm = kept("table_warm", [P, 1], F32)
+        nc.scalar.activation(out=table_warm[:], in_=ident_f[:, 0:1], func=ACT.Tanh)
+        load_tokens(xl_sb, xl, "xl", 0)
         load_v(0, 1)
-        load_rows(xl_sb, xl, "xl", 1)
-        load_v(1, 0)
-        load_v(1, 1)
-        load_v(2, 0)
-        load_v(2, 1)
+        load_tokens(xl_sb, xl, "xl", 1)
+        for e in (1, 2):
+            load_v(e, 0)
+            load_v(e, 1)
         load_u(0)
         load_v(3, 0)
         load_v(3, 1)
         for e in range(1, E):
             load_u(e)
-        load_rows(x0_sb, x0, "x0", 0)
-        load_rows(x0_sb, x0, "x0", 1)
+        load_tokens(x0_sb, x0, "x0", 0)
+        load_tokens(x0_sb, x0, "x0", 1)
 
-        grouped, codes, scales = {}, {}, {}
+        laid, codes, scales = {}, {}, {}
 
-        def quant(*keys):
-            name = "%s%d%d" % keys[0]
-            whole, first = home[keys[0]]
-            width = grouped[keys[0]].shape[1] // PACK
-            code_tile = kept("c_" + name, [P, len(keys) * width], U32)
-            scale_tile = kept("s_" + name, [P, len(keys) * width], U8)
-            nc.vector.quantize_mx(out=code_tile[:].bitcast(FP8X4), scales=scale_tile[:],
-                                  in_=whole[:, first:first + len(keys) * width * PACK])
-            for n, key in enumerate(keys):
-                assert home[key] == (whole, first + n * width * PACK)
-                codes[key] = code_tile[:, n * width:(n + 1) * width]
-                scales[key] = scale_tile[:, n * width:(n + 1) * width]
+        def make_room(key, tag, bufs, width):
+            tile = ring.tile([P, width], BF16, name=tag, tag=tag, bufs=bufs, align_bytes=64)
+            laid[key] = tile[:]
 
-        home = {}
+        def quant(key):
+            words = laid[key].shape[1] // PACK
+            code_tile = kept("c_%s%d%d" % key, [P, words], U32)
+            scale_tile = kept("s_%s%d%d" % key, [P, words], U8)
+            nc.vector.quantize_mx(out=code_tile[:].bitcast(FP8X4), scales=scale_tile[:], in_=laid[key])
+            codes[key], scales[key] = code_tile[:], scale_tile[:]
 
-        def room(tag, bufs, width, *keys):
-            whole = ring.tile([P, len(keys) * width], BF16, name=tag, tag=tag, bufs=bufs, align_bytes=64)
-            for n, key in enumerate(keys):
-                home[key] = (whole, n * width)
-                grouped[key] = whole[:, n * width:(n + 1) * width]
+        def weight_room(key):
+            make_room(key, "laid", 5, KP * PACK)
 
-        def x_turn(bt):
-            words = xl_sb[bt // 2][:, bt % 2, :].bitcast(F32)
-            turned = bank("mm", [P, NH * 2, P], F32)
-            for g in range(NH):
-                for w in range(2):
-                    nc.tensor.transpose(turned[:, 2 * g + w, :], words[:, 256 * g + w:256 * (g + 1):2], ident_f[:])
-            room("xg", NT, NH * P * PACK, ("x", bt, 0))
-            nc.scalar.copy(out=grouped["x", bt, 0][:].bitcast(F32).rearrange("p (g b w) -> p g b w", g=NH, w=2),
-                           in_=turned[:].rearrange("p (g w) b -> p g b w", w=2))
+        def handover_room(key):
+            make_room(key, "handover", 1, KP * PACK)
 
         def pool_copy(out, in_):
             nc.gpsimd.tensor_scalar(out=out, in0=in_, scalar1=1.0, scalar2=0.0, op0=ALU.mult, op1=ALU.add)
 
-        def direct(kind, e, i, engine, lo=0, hi=NQ):
-            if (kind, e, i) not in grouped:
-                room("grouped", 5, KP * PACK, (kind, e, i))
-            dst = grouped[kind, e, i]
-            copy = {"vector": nc.vector.tensor_copy, "scalar": nc.scalar.copy, "gpsimd": pool_copy}[engine]
-            if engine == "gpsimd" and kind == "u":
-                copy(out=dst.rearrange("p (c j) -> p c j", j=PACK)[:, lo * 32:hi * 32], in_=raw[kind, e, i].rearrange("p j c -> p c j")[:, lo * 32:hi * 32])
-            elif kind == "v":
-                copy(out=dst.rearrange("p (t q r j) -> p q t r j", t=PACK, r=RUN, j=PACK)[:, lo:hi],
-                     in_=raw[kind, e, i].rearrange("p j (q t r) -> p q t r j", t=PACK, r=RUN)[:, lo:hi])
-            else:
-                copy(out=dst.rearrange("p (c i j) -> p c j i", i=4, j=PACK)[:, lo * 8:hi * 8], in_=raw[kind, e, i].rearrange("p j (c i) -> p c j i", i=4)[:, lo * 8:hi * 8])
+        def lay_v(key, copy, lo=0, hi=NQ):
+            copy(out=laid[key].rearrange("p (t q i j) -> p q t i j", t=PACK, i=RUN, j=PACK)[:, lo:hi],
+                 in_=raw[key].rearrange("p j (q t i) -> p q t i j", t=PACK, i=RUN)[:, lo:hi])
 
-        def route(kind, e, i):
-            if (kind, e, i) not in grouped:
-                room("grouped", 5, KP * PACK, (kind, e, i))
-            dst = grouped[kind, e, i]
-            src = raw[kind, e, i].rearrange("p j c -> p c j")
-            for half in range(2):
-                laid = bank("turn", [P, 2 * KP], BF16)
+        def lay_u_on_pool(key):
+            pool_copy(out=laid[key].rearrange("p (c j) -> p c j", j=PACK), in_=raw[key].rearrange("p j c -> p c j"))
+
+        def lay_u_on_scalar(key):
+            nc.scalar.copy(out=laid[key].rearrange("p (c n j) -> p c j n", n=NEAR, j=PACK),
+                           in_=raw[key].rearrange("p j (c n) -> p c j n", n=NEAR))
+
+        def lay_u_on_tensor(key):
+            weight_room(key)
+            src = raw[key].rearrange("p j c -> p c j")
+            for part in range(2):
+                streamed = bank("turn", [P, 2 * KP], BF16)
                 for k in range(2):
-                    c0 = (2 * half + k) * P
-                    nc.tensor.matmul(out=laid[:, k * KP:(k + 1) * KP].rearrange("p (c j) -> p c j", j=PACK), lhsT=ident_b[:],
+                    c0 = (2 * part + k) * P
+                    nc.tensor.matmul(out=streamed[:, k * KP:(k + 1) * KP].rearrange("p (c j) -> p c j", j=PACK), lhsT=ident_b[:],
                                      rhs=src[:, c0:c0 + P, :], start=True, stop=True)
-                if kind == "v":
-                    nc.scalar.copy(out=dst.bitcast(F32).rearrange("p (t q w) -> p q t w", t=PACK, q=NQ)[:, half * RUN:(half + 1) * RUN],
-                                   in_=laid[:].bitcast(F32).rearrange("p (q t w) -> p q t w", t=PACK, q=RUN))
-                else:
-                    nc.scalar.copy(out=dst[:, half * 2 * KP:(half + 1) * 2 * KP].bitcast(F32), in_=laid[:].bitcast(F32))
+                nc.scalar.copy(out=laid[key][:, part * 2 * KP:(part + 1) * 2 * KP].bitcast(F32), in_=streamed[:].bitcast(F32))
 
-        tanh_h = {}
+        def turn_words(rows):
+            words = rows.bitcast(F32)
+            turned = bank("product", [P, NH * 2, P], F32)
+            for g in range(NH):
+                for w in range(2):
+                    nc.tensor.transpose(turned[:, 2 * g + w, :], words[:, 256 * g + w:256 * (g + 1):2], ident_f[:])
+            return turned
+
+        def x_turn(bt):
+            turned = turn_words(xl_sb[bt // 2][:, bt % 2, :])
+            make_room(("x", bt, 0), "x_laid", NT, NH * KP)
+            nc.scalar.copy(out=laid["x", bt, 0].bitcast(F32).rearrange("p (g b w) -> p g b w", g=NH, w=2),
+                           in_=turned[:].rearrange("p (g w) b -> p g b w", w=2))
+
+        gw_cols = kept("gw_cols", [P, E, NH, PACK], BF16)
+
+        def gate_turn():
+            turned = turn_words(small_rows[:])
+            nc.scalar.copy(out=gw_cols[:].rearrange("p e g t -> p e (g t)").bitcast(F32), in_=turned[:, :, 0:E].rearrange("p w e -> p e w"))
+
+        s_sorted = kept("s_sorted", [P, PACK, P], F32)
+        gains = bank("gain", [P, PACK, P], F32)
+
+        def gain_sort():
+            nc.scalar.copy(out=s_sorted[:].rearrange("e t (q i) -> e t q i", i=RUN),
+                           in_=small_rows[:, 0:R].rearrange("e (q t i) -> e t q i", t=PACK, i=RUN))
+
+        def gain_turn():
+            for t in range(PACK):
+                nc.tensor.transpose(gains[:, t, :], s_sorted[:, t, :], ident_f[:])
+
+        tanh_h, p_laid = {}, {}
 
         def hidden(e, bt):
-            hb = bank("mm", [P, PACK, P], F32)
+            hb = bank("product", [P, PACK, P], F32)
             for t in range(PACK):
                 for g in range(NH):
                     nc.tensor.matmul_mx(out=hb[:, t, :],
@@ -191,64 +176,69 @@ def tile_crossnetlowrankmixture_x1_kernel(tc, x0, xl, v, s, u, gw, out_0, out_1,
                                         rhs=codes["x", bt, 0][:, g * P:(g + 1) * P].bitcast(FP8X4), rhs_scale=scales["x", bt, 0][:, g * P:(g + 1) * P],
                                         start=(g == 0), stop=(g == NH - 1))
             if bt == 0:
-                tanh_h[e] = ring.tile([P, B, PACK], F32, name="tanh_h", tag="tanh_h", bufs=2, align_bytes=64)
+                tanh_h[e] = ring.tile([P, B, PACK], F32, name="tanh_h", tag="tanh_h", align_bytes=64)
             nc.scalar.activation(out=tanh_h[e][:, bt * P:(bt + 1) * P, :], in_=hb[:].rearrange("p t b -> p b t"), func=ACT.Tanh)
 
-        def gain(e, *pairs):
-            if pairs[0] == 0:
-                room("pg", 2, 2 * KP, ("p", e, 0), ("p", e, 1))
-            whole, first = home["p", e, pairs[0]]
-            n = 2 * P * len(pairs)
-            nc.vector.tensor_tensor(out=whole[:, first:first + n * PACK].rearrange("p (b t) -> p b t", t=PACK),
-                                    in0=tanh_h[e][:, pairs[0] * 2 * P:pairs[0] * 2 * P + n, :],
-                                    in1=gains[:, :, E + e:E + e + 1].rearrange("p t o -> p o t").to_broadcast([P, n, PACK]), op=ALU.mult)
+        def gain(e, pair):
+            if pair == 0:
+                p_laid[e] = ring.tile([P, B * PACK], BF16, name="p_laid", tag="p_laid", align_bytes=64)
+            laid["p", e, pair] = p_laid[e][:, pair * 2 * KP:(pair + 1) * 2 * KP]
+            nc.vector.tensor_tensor(out=laid["p", e, pair].rearrange("p (b t) -> p b t", t=PACK),
+                                    in0=tanh_h[e][:, pair * 2 * P:(pair + 1) * 2 * P, :],
+                                    in1=gains[:, :, E + e:E + e + 1].rearrange("p t o -> p o t").to_broadcast([P, 2 * P, PACK]), op=ALU.mult)
 
-        gate = kept("gate", [P, NT, E], F32)
         logit = bank("gate", [P, NT, E], F32)
-
-        def logits(bt, step):
-            xg = grouped["x", bt, 0][:].rearrange("p (g b t) -> p g b t", g=NH, t=PACK)
-            for n in (2 * step, 2 * step + 1):
-                g, t = divmod(n, PACK)
-                nc.tensor.matmul(out=logit[:, bt, :], lhsT=xg[:, g, :, t], rhs=cols[:, :, g, t], start=(n == 0), stop=(n == NH * PACK - 1))
-
+        logit_steps = [(bt, n) for bt in range(NT) for n in range(NH * PACK)]
         top = kept("top", [P, NT], F32)
         shifted = kept("shifted", [P, NT, E], F32)
         total = kept("total", [P, NT], F32)
-        inv = kept("inv", [P, NT], F32)
+        inverse = kept("inverse", [P, NT], F32)
+        gate = kept("gate", [P, NT, E], F32)
 
-        def soft(step):
-            if step == 0:
-                nc.vector.tensor_reduce(out=top[:], in_=logit[:], axis=AX.X, op=ALU.max)
-            elif step == 1:
-                nc.vector.tensor_tensor(out=shifted[:], in0=logit[:], in1=top[:].unsqueeze(2).to_broadcast([P, NT, E]), op=ALU.subtract)
-                nc.scalar.activation(out=shifted[:], in_=shifted[:], func=ACT.Exp)
-            elif step == 2:
-                nc.vector.tensor_reduce(out=total[:], in_=shifted[:], axis=AX.X, op=ALU.add)
-            elif step == 3:
-                nc.vector.reciprocal(out=inv[:], in_=total[:])
-            else:
-                nc.vector.tensor_tensor(out=gate[:], in0=shifted[:], in1=inv[:].unsqueeze(2).to_broadcast([P, NT, E]), op=ALU.mult)
+        def logits(steps):
+            for bt, n in steps:
+                g, t = divmod(n, PACK)
+                x_cols = laid["x", bt, 0].rearrange("p (g b t) -> p g b t", g=NH, t=PACK)
+                nc.tensor.matmul(out=logit[:, bt, :], lhsT=x_cols[:, g, :, t], rhs=gw_cols[:, :, g, t], start=(n == 0), stop=(n == NH * PACK - 1))
+
+        def gate_max():
+            nc.vector.tensor_reduce(out=top[:], in_=logit[:], axis=AX.X, op=ALU.max)
+
+        def gate_exp():
+            nc.vector.tensor_tensor(out=shifted[:], in0=logit[:], in1=top[:].unsqueeze(2).to_broadcast([P, NT, E]), op=ALU.subtract)
+            nc.scalar.activation(out=shifted[:], in_=shifted[:], func=ACT.Exp)
+
+        def gate_sum():
+            nc.vector.tensor_reduce(out=total[:], in_=shifted[:], axis=AX.X, op=ALU.add)
+
+        def gate_inverse():
+            nc.vector.reciprocal(out=inverse[:], in_=total[:])
+
+        def gate_scale():
+            nc.vector.tensor_tensor(out=gate[:], in0=shifted[:], in1=inverse[:].unsqueeze(2).to_broadcast([P, NT, E]), op=ALU.mult)
 
         acc = {}
         for h in range(NH):
             for pair in range(2):
                 acc[h, pair] = kept("acc%d%d" % (h, pair), [P, 2, KP], F32)
 
+        def tiles_of(by_pair, bts):
+            return by_pair[:, bts[0] % 2:bts[-1] % 2 + 1, :]
+
         def mix(e, h, bt):
-            qb = bank("mm", [P, KP], F32)
+            qb = bank("product", [P, KP], F32)
             span = slice((bt % 2) * P, (bt % 2 + 1) * P)
             nc.tensor.matmul_mx(out=qb[:], lhsT=codes["p", e, bt // 2][:, span].bitcast(FP8X4), lhsT_scale=scales["p", e, bt // 2][:, span],
-                                rhs=codes["u", e, h][:].bitcast(FP8X4), rhs_scale=scales["u", e, h][:], start=True, stop=True)
+                                rhs=codes["u", e, h].bitcast(FP8X4), rhs_scale=scales["u", e, h], start=True, stop=True)
             dst = acc[h, bt // 2][:, bt % 2, :]
             if e == 0:
                 nc.scalar.activation(out=dst, in_=qb[:], func=ACT.Copy, scale=gate[:, bt, 0:1])
             else:
                 nc.vector.scalar_tensor_tensor(out=dst, in0=qb[:], scalar=gate[:, bt, e:e + 1], in1=dst, op0=ALU.mult, op1=ALU.add)
 
-        def times_x0(h, bts, engine=nc.vector):
-            dst = acc[h, bts[0] // 2][:, bts[0] % 2:bts[-1] % 2 + 1, :]
-            engine.tensor_tensor(out=dst, in0=dst, in1=x0_sb[bts[0] // 2][:, bts[0] % 2:bts[-1] % 2 + 1, h * KP:(h + 1) * KP], op=ALU.mult)
+        def times_x0(h, bts, engine):
+            dst = tiles_of(acc[h, bts[0] // 2], bts)
+            engine.tensor_tensor(out=dst, in0=dst, in1=tiles_of(x0_sb[bts[0] // 2], bts)[:, :, h * KP:(h + 1) * KP], op=ALU.mult)
 
         def plus_xl(h, bt, engine):
             dst = acc[h, bt // 2][:, bt % 2, :]
@@ -257,28 +247,19 @@ def tile_crossnetlowrankmixture_x1_kernel(tc, x0, xl, v, s, u, gw, out_0, out_1,
 
         rounded_words = {}
 
-        def plus_xl_rounded(h, bt):
-            rounded = ring.tile([P, 1, 2, P, 2], BF16, name="rounded", tag="rounded", bufs=2, align_bytes=64)
-            nc.vector.tensor_tensor(out=rounded[:, 0], in0=acc[h, bt // 2][:, bt % 2, :].rearrange("b (p w i) -> b w p i", w=2, i=2),
-                                    in1=xl_sb[bt // 2][:, bt % 2, h * KP:(h + 1) * KP].rearrange("b (p w i) -> b w p i", w=2, i=2), op=ALU.add)
-            rounded_words[h, (bt,)] = rounded[:].rearrange("b n w p i -> b (n w p i)").bitcast(F32)
-
         def out_round(h, bts):
-            n = len(bts)
-            rounded = ring.tile([P, n, 2, P, 2], BF16, name="rounded", tag="rounded", bufs=2, align_bytes=64)
-            src = acc[h, bts[0] // 2][:, bts[0] % 2:bts[-1] % 2 + 1, :]
-            nc.scalar.copy(out=rounded[:], in_=src.rearrange("b n (p w i) -> b n w p i", w=2, i=2))
+            rounded = ring.tile([P, len(bts), 2, P, 2], BF16, name="rounded", tag="rounded", align_bytes=64)
+            nc.scalar.copy(out=rounded[:], in_=tiles_of(acc[h, bts[0] // 2], bts).rearrange("b n (p w i) -> b n w p i", w=2, i=2))
             rounded_words[h, bts] = rounded[:].rearrange("b n w p i -> b (n w p i)").bitcast(F32)
 
         def out_turn(h, bts):
             n = len(bts)
-            words = rounded_words[h, bts]
             turned = bank("turn", [P, n, 2, P], F32)
-            for i in range(n):
+            for k in range(n):
                 for w in range(2):
-                    nc.tensor.transpose(turned[:, i, w, :], words[:, (2 * i + w) * P:(2 * i + w + 1) * P], ident_f[:])
-            grouped["o", h, bts[0]] = ring.tile([P, n * KP], BF16, name="og", tag="og", bufs=3, align_bytes=64)
-            nc.scalar.copy(out=grouped["o", h, bts[0]][:].bitcast(F32).rearrange("p (n b w) -> p n b w", n=n, w=2),
+                    nc.tensor.transpose(turned[:, k, w, :], rounded_words[h, bts][:, (2 * k + w) * P:(2 * k + w + 1) * P], ident_f[:])
+            make_room(("o", h, bts), "out_laid", 3, n * KP)
+            nc.scalar.copy(out=laid["o", h, bts].bitcast(F32).rearrange("p (n b w) -> p n b w", n=n, w=2),
                            in_=turned[:].rearrange("p n w b -> p n b w"))
 
         out_scales = [kept("out_scales%d" % h, [P, B], U8) for h in range(NH)]
@@ -286,112 +267,125 @@ def tile_crossnetlowrankmixture_x1_kernel(tc, x0, xl, v, s, u, gw, out_0, out_1,
         def out_quant(h, bts):
             span = slice(bts[0] * P, (bts[-1] + 1) * P)
             words = kept("out_words%d%d" % (h, bts[0]), [P, len(bts) * P], I32)
-            nc.vector.quantize_mx(out=words[:].bitcast(FP8X4), scales=out_scales[h][:, span],
-                                  in_=grouped["o", h, bts[0]][:])
+            nc.vector.quantize_mx(out=words[:].bitcast(FP8X4), scales=out_scales[h][:, span], in_=laid["o", h, bts])
             nc.sync.dma_start(out=out_1[h].rearrange("p m t -> p (m t)").bitcast(I32)[:, span], in_=words[:])
             if bts[-1] == NT - 1:
-                for q in range(4):
-                    queue = nc.scalar if (h == NH - 1 and q % 2) else nc.sync
-                    queue.dma_start(out=out_2[h, 4 * q:4 * q + 4, :].bitcast(I32), in_=out_scales[h][32 * q:32 * q + 4, :].bitcast(I32))
+                for n in range(P // 32):
+                    queue = nc.scalar if (h == NH - 1 and n % 2) else nc.sync
+                    queue.dma_start(out=out_2[h, 4 * n:4 * n + 4, :].bitcast(I32), in_=out_scales[h][32 * n:32 * n + 4, :].bitcast(I32))
 
-        def handover(key):
-            room("handover", 1, KP * PACK, key)
+        def lay_v_on_vector(e, g):
+            weight_room(("v", e, g))
+            lay_v(("v", e, g), nc.vector.tensor_copy)
 
-        ADD = nc.gpsimd
-        units = [(h, (2 * pair, 2 * pair + 1)) for h in range(NH) for pair in range(2)]
-        direct("v", 0, 0, "vector")
+        lay_v_on_vector(0, 0)
         gain_sort()
         x_turn(0)
         x_turn(1)
         quant(("v", 0, 0))
-        direct("v", 0, 1, "vector")
+        lay_v_on_vector(0, 1)
         quant(("x", 0, 0))
         quant(("v", 0, 1))
         quant(("x", 1, 0))
-        gain_turn()
-        direct("v", 1, 0, "vector")
+        x_turn(2)
+        lay_v_on_vector(1, 0)
         hidden(0, 0)
         hidden(0, 1)
-        x_turn(2)
-        x_turn(3)
-        quant(("v", 1, 0))
-        route("v", 1, 1)
-        handover(("v", 2, 0))
-        direct("v", 2, 0, "vector")
         quant(("x", 2, 0))
-        quant(("x", 3, 0))
+        x_turn(3)
         hidden(0, 2)
+        handover_room(("v", 2, 0))
+        lay_v(("v", 2, 0), nc.scalar.copy, NQ // 2, NQ)
+        lay_v_on_vector(1, 1)
+        quant(("v", 1, 0))
+        quant(("x", 3, 0))
         hidden(0, 3)
+        gain_turn()
+        lay_v(("v", 2, 0), nc.vector.tensor_copy, 0, NQ // 2)
         gate_turn()
-        by_pool = [("v", 2, 1), ("v", 3, 1), ("u", 2, 0), ("u", 3, 0), ("u", 0, 1)]
-        by_scalar = [("v", 3, 0), ("u", 0, 0), ("u", 1, 0)]
         quant(("v", 1, 1))
         quant(("v", 2, 0))
+
+        on_pool = [("v", 2, 1), ("v", 3, 1), ("u", 2, 0), ("u", 3, 0)]
+        on_scalar = [("v", 3, 0), ("u", 0, 0), ("u", 1, 0)]
+        gate_round = 2
         for e in range(E):
-            handover(by_pool[e])
-            direct(*by_pool[e], "gpsimd")
+            handover_room(on_pool[e])
+            if on_pool[e][0] == "v":
+                lay_v(on_pool[e], pool_copy)
+            else:
+                lay_u_on_pool(on_pool[e])
             gain(e, 0)
-            if e == 2:
-                soft(0)
+            if e == gate_round:
+                gate_max()
             gain(e, 1)
-            if e == 2:
-                soft(1)
+            if e == gate_round:
+                gate_exp()
             if e + 1 < E:
                 for bt in range(NT):
                     hidden(e + 1, bt)
-                    if e < 2:
-                        logits(2 * e + bt // 2, 2 * (bt % 2))
-                        logits(2 * e + bt // 2, 2 * (bt % 2) + 1)
-                direct(*by_scalar[e], "scalar")
-            if e == 3:
-                rotation["mm"] = rotation["mm"] + rotation["gate"] + rotation["gain"]
+                    first = (e * NT + bt) * LOGITS_PER_TILE
+                    logits(logit_steps[first:first + LOGITS_PER_TILE])
+                weight_room(on_scalar[e])
+                if on_scalar[e][0] == "v":
+                    lay_v(on_scalar[e], nc.scalar.copy)
+                else:
+                    lay_u_on_scalar(on_scalar[e])
+            else:
+                rotation["product"] = rotation["product"] + rotation["gate"] + rotation["gain"]
                 for bt in range(NT):
                     mix(0, 0, bt)
-                route("u", 1, 1)
+                lay_u_on_tensor(("u", 1, 1))
             quant(("p", e, 0))
-            if e == 2:
-                soft(2)
+            if e == gate_round:
+                gate_sum()
             quant(("p", e, 1))
-            if e == 2:
-                soft(3)
+            if e == gate_round:
+                gate_inverse()
             if e > 0:
-                quant(by_scalar[e - 1])
-            if e == 2:
-                soft(4)
-            quant(by_pool[e])
-        handover(by_pool[E])
-        direct(*by_pool[E], "gpsimd")
+                quant(on_scalar[e - 1])
+            if e == gate_round:
+                gate_scale()
+            quant(on_pool[e])
+        handover_room(("u", 0, 1))
+        lay_u_on_pool(("u", 0, 1))
 
+        units = [(h, (2 * pair, 2 * pair + 1)) for h in range(NH) for pair in range(2)]
+        last = len(units) - 1
         for k, (h, bts) in enumerate(units):
             for e in range(1, E):
                 for bt in bts:
                     mix(e, h, bt)
                 if e == 2 and k == 1:
-                    route("u", 3, 1)
+                    lay_u_on_tensor(("u", 3, 1))
                 if e == 2 and k >= 2:
                     out_turn(*units[k - 2])
             if k == 0:
                 quant(("u", 1, 1))
-                route("u", 2, 1)
+                lay_u_on_tensor(("u", 2, 1))
             if k == 1:
-                quant(("u", 0, 1))
-                quant(("u", 2, 1))
-                quant(("u", 3, 1))
-            if 0 < k < len(units) - 1:
+                for e in (0, 2, 3):
+                    quant(("u", e, 1))
+            if 0 < k < last:
                 for bt in units[k + 1][1]:
                     mix(0, units[k + 1][0], bt)
             if k >= 1:
                 out_round(*units[k - 1])
             if k >= 2:
                 out_quant(*units[k - 2])
-            if k + 1 < len(units):
-                times_x0(h, bts)
+            if k < last - 1:
+                times_x0(h, bts[1:], nc.vector)
+                plus_xl(h, bts[1], nc.gpsimd)
+                times_x0(h, bts[:1], nc.gpsimd)
+                plus_xl(h, bts[0], nc.gpsimd)
+            elif k < last:
+                times_x0(h, bts, nc.vector)
                 for bt in bts:
-                    plus_xl(h, bt, ADD)
+                    plus_xl(h, bt, nc.gpsimd)
             else:
                 out_turn(*units[k - 1])
                 for bt in bts:
-                    times_x0(h, (bt,))
+                    times_x0(h, (bt,), nc.vector)
                 for bt in bts:
                     plus_xl(h, bt, nc.vector)
                     out_round(h, (bt,))

@@ -24,6 +24,7 @@ NH = D // KP
 RUN = 8
 NQ = P // RUN
 NEAR = 4
+POOL_BLOCKS = 14
 LOGITS_PER_TILE = 4
 
 
@@ -46,7 +47,7 @@ def tile_crossnetlowrankmixture_x1_kernel(tc, x0, xl, v, s, u, gw, out_0, out_1,
             return psum.tile(shape, dtype, name=tag, tag=tag)
 
         small_rows = kept("small_rows", [P, D], BF16)
-        nc.gpsimd.memset(small_rows[:].bitcast(F32), 0.0)
+        nc.vector.memset(small_rows[:].bitcast(F32), 0.0)
         ident_f = kept("ident_f", [P, P], F32)
         ident_b = kept("ident_b", [P, P], BF16)
         make_identity(nc, ident_f[:])
@@ -71,24 +72,20 @@ def tile_crossnetlowrankmixture_x1_kernel(tc, x0, xl, v, s, u, gw, out_0, out_1,
             dst[pair] = kept("%s%d" % (name, pair), [P, 2, D], BF16)
             nc.sync.dma_start(out=dst[pair][:], in_=src[pair * 2 * P:(pair + 1) * 2 * P, :].rearrange("(n p) d -> p n d", p=P))
 
-        load_v(0, 0)
+        for n in range(2):
+            load_v(0, n)
+            load_tokens(xl_sb, xl, "xl", n)
         nc.sync.dma_start(out=small_rows[0:E, :], in_=gw)
         nc.sync.dma_start(out=small_rows[E:2 * E, 0:R], in_=s)
-        table_warm = kept("table_warm", [P, 1], F32)
-        nc.scalar.activation(out=table_warm[:], in_=ident_f[:, 0:1], func=ACT.Tanh)
-        load_tokens(xl_sb, xl, "xl", 0)
-        load_v(0, 1)
-        load_tokens(xl_sb, xl, "xl", 1)
-        for e in (1, 2):
-            load_v(e, 0)
-            load_v(e, 1)
-        load_u(0)
-        load_v(3, 0)
-        load_v(3, 1)
-        for e in range(1, E):
+        for e, g in ((1, 0), (1, 1), (2, 0), (2, 1), (3, 1), (3, 0)):
+            load_v(e, g)
+        for e in (2, 0, 1, 3):
             load_u(e)
         load_tokens(x0_sb, x0, "x0", 0)
         load_tokens(x0_sb, x0, "x0", 1)
+
+        table_warm = kept("table_warm", [P, 1], F32)
+        nc.scalar.activation(out=table_warm[:], in_=ident_f[:, 0:1], func=ACT.Tanh)
 
         laid, codes, scales = {}, {}, {}
 
@@ -116,8 +113,9 @@ def tile_crossnetlowrankmixture_x1_kernel(tc, x0, xl, v, s, u, gw, out_0, out_1,
             copy(out=laid[key].rearrange("p (t q i j) -> p q t i j", t=PACK, i=RUN, j=PACK)[:, lo:hi],
                  in_=raw[key].rearrange("p j (q t i) -> p q t i j", t=PACK, i=RUN)[:, lo:hi])
 
-        def lay_u_on_pool(key):
-            pool_copy(out=laid[key].rearrange("p (c j) -> p c j", j=PACK), in_=raw[key].rearrange("p j c -> p c j"))
+        def lay_u(key, copy, lo=0, hi=NQ):
+            cols = slice(lo * RUN * PACK, hi * RUN * PACK)
+            copy(out=laid[key].rearrange("p (c j) -> p c j", j=PACK)[:, cols], in_=raw[key].rearrange("p j c -> p c j")[:, cols])
 
         def lay_u_on_scalar(key):
             nc.scalar.copy(out=laid[key].rearrange("p (c n j) -> p c j n", n=NEAR, j=PACK),
@@ -236,9 +234,9 @@ def tile_crossnetlowrankmixture_x1_kernel(tc, x0, xl, v, s, u, gw, out_0, out_1,
             else:
                 nc.vector.scalar_tensor_tensor(out=dst, in0=qb[:], scalar=gate[:, bt, e:e + 1], in1=dst, op0=ALU.mult, op1=ALU.add)
 
-        def times_x0(h, bts, engine):
+        def times_x0(h, bts):
             dst = tiles_of(acc[h, bts[0] // 2], bts)
-            engine.tensor_tensor(out=dst, in0=dst, in1=tiles_of(x0_sb[bts[0] // 2], bts)[:, :, h * KP:(h + 1) * KP], op=ALU.mult)
+            nc.vector.tensor_tensor(out=dst, in0=dst, in1=tiles_of(x0_sb[bts[0] // 2], bts)[:, :, h * KP:(h + 1) * KP], op=ALU.mult)
 
         def plus_xl(h, bt, engine):
             dst = acc[h, bt // 2][:, bt % 2, :]
@@ -279,7 +277,6 @@ def tile_crossnetlowrankmixture_x1_kernel(tc, x0, xl, v, s, u, gw, out_0, out_1,
             lay_v(("v", e, g), nc.vector.tensor_copy)
 
         lay_v_on_vector(0, 0)
-        gain_sort()
         x_turn(0)
         x_turn(1)
         quant(("v", 0, 0))
@@ -290,6 +287,7 @@ def tile_crossnetlowrankmixture_x1_kernel(tc, x0, xl, v, s, u, gw, out_0, out_1,
         x_turn(2)
         lay_v_on_vector(1, 0)
         hidden(0, 0)
+        gain_sort()
         hidden(0, 1)
         quant(("x", 2, 0))
         x_turn(3)
@@ -311,10 +309,8 @@ def tile_crossnetlowrankmixture_x1_kernel(tc, x0, xl, v, s, u, gw, out_0, out_1,
         gate_round = 2
         for e in range(E):
             handover_room(on_pool[e])
-            if on_pool[e][0] == "v":
-                lay_v(on_pool[e], pool_copy)
-            else:
-                lay_u_on_pool(on_pool[e])
+            lay = lay_v if on_pool[e][0] == "v" else lay_u
+            lay(on_pool[e], pool_copy, 0, POOL_BLOCKS)
             gain(e, 0)
             if e == gate_round:
                 gate_max()
@@ -336,6 +332,7 @@ def tile_crossnetlowrankmixture_x1_kernel(tc, x0, xl, v, s, u, gw, out_0, out_1,
                 for bt in range(NT):
                     mix(0, 0, bt)
                 lay_u_on_tensor(("u", 1, 1))
+            lay(on_pool[e], nc.vector.tensor_copy, POOL_BLOCKS, NQ)
             quant(("p", e, 0))
             if e == gate_round:
                 gate_sum()
@@ -348,7 +345,7 @@ def tile_crossnetlowrankmixture_x1_kernel(tc, x0, xl, v, s, u, gw, out_0, out_1,
                 gate_scale()
             quant(on_pool[e])
         handover_room(("u", 0, 1))
-        lay_u_on_pool(("u", 0, 1))
+        lay_u(("u", 0, 1), pool_copy)
 
         units = [(h, (2 * pair, 2 * pair + 1)) for h in range(NH) for pair in range(2)]
         last = len(units) - 1
@@ -373,19 +370,14 @@ def tile_crossnetlowrankmixture_x1_kernel(tc, x0, xl, v, s, u, gw, out_0, out_1,
                 out_round(*units[k - 1])
             if k >= 2:
                 out_quant(*units[k - 2])
-            if k < last - 1:
-                times_x0(h, bts[1:], nc.vector)
-                plus_xl(h, bts[1], nc.gpsimd)
-                times_x0(h, bts[:1], nc.gpsimd)
-                plus_xl(h, bts[0], nc.gpsimd)
-            elif k < last:
-                times_x0(h, bts, nc.vector)
+            if k < last:
+                times_x0(h, bts)
                 for bt in bts:
                     plus_xl(h, bt, nc.gpsimd)
             else:
                 out_turn(*units[k - 1])
                 for bt in bts:
-                    times_x0(h, (bt,), nc.vector)
+                    times_x0(h, (bt,))
                 for bt in bts:
                     plus_xl(h, bt, nc.vector)
                     out_round(h, (bt,))

from contextlib import ExitStack

import concourse.mybir as mybir
from concourse.masks import make_identity

B, D, R, E = 512, 1024, 512, 4
FLOPS = 2 * E * B * D * R * 2

F32 = mybir.dt.float32
BF16 = mybir.dt.bfloat16
U32 = mybir.dt.uint32
I32 = mybir.dt.int32
U8 = mybir.dt.uint8
FP8X4 = mybir.dt.float8_e4m3fn_x4
ACT = mybir.ActivationFunctionType
ALU = mybir.AluOpType
AX = mybir.AxisListType

P = 128
PACK = 4
KP = P * PACK
NT = B // P
NH = D // KP
RUN = 8
NQ = P // RUN
NEAR = 4
POOL_BLOCKS = 14
LOGITS_PER_TILE = 4


def tile_crossnetlowrankmixture_x1_kernel(tc, x0, xl, v, s, u, gw, out_0, out_1, out_2):
    nc = tc.nc
    with ExitStack() as ctx:
        keep = ctx.enter_context(tc.tile_pool(name="keep", bufs=1))
        ring = ctx.enter_context(tc.tile_pool(name="ring", bufs=2))
        psum = ctx.enter_context(tc.psum_pool(name="psum", bufs=1))
        ctx.enter_context(tc.manual_schedule())

        def kept(name, shape, dtype):
            return keep.tile(shape, dtype, name=name, align_bytes=64)

        rotation = {"turn": ["b0", "b1"], "product": ["b2", "b3", "b4", "b5"], "gate": ["b6"], "gain": ["b7"]}

        def bank(role, shape, dtype):
            tag = rotation[role][0]
            rotation[role] = rotation[role][1:] + [tag]
            return psum.tile(shape, dtype, name=tag, tag=tag)

        small_rows = kept("small_rows", [P, D], BF16)
        nc.vector.memset(small_rows[:].bitcast(F32), 0.0)
        ident_f = kept("ident_f", [P, P], F32)
        ident_b = kept("ident_b", [P, P], BF16)
        make_identity(nc, ident_f[:])
        make_identity(nc, ident_b[:])

        raw, xl_sb, x0_sb = {}, {}, {}

        def load_v(e, g):
            tile = kept("v_raw%d%d" % (e, g), [P, PACK, R], BF16)
            raw["v", e, g] = tile[:]
            nc.sync.dma_start(out=tile[:], in_=v[e, g * KP:(g + 1) * KP, :].rearrange("(p j) c -> p j c", j=PACK))

        def load_u(e):
            tile = kept("u_raw%d" % e, [P, PACK, D], BF16)
            rows_by_value = u[e].rearrange("(q t i) d -> t q i d", t=PACK, i=RUN)
            for t in range(PACK):
                nc.sync.dma_start(out=tile[:, t, :], in_=rows_by_value[t])
            for h in range(NH):
                raw["u", e, h] = tile[:, :, h * KP:(h + 1) * KP]

        def load_tokens(dst, src, name, pair):
            dst[pair] = kept("%s%d" % (name, pair), [P, 2, D], BF16)
            nc.sync.dma_start(out=dst[pair][:], in_=src[pair * 2 * P:(pair + 1) * 2 * P, :].rearrange("(n p) d -> p n d", p=P))

        for n in range(2):
            load_v(0, n)
            load_tokens(xl_sb, xl, "xl", n)
        nc.sync.dma_start(out=small_rows[0:E, :], in_=gw)
        nc.sync.dma_start(out=small_rows[E:2 * E, 0:R], in_=s)
        for e, g in ((1, 0), (1, 1), (2, 0), (2, 1), (3, 1), (3, 0)):
            load_v(e, g)
        for e in (2, 0, 1, 3):
            load_u(e)
        load_tokens(x0_sb, x0, "x0", 0)
        load_tokens(x0_sb, x0, "x0", 1)

        table_warm = kept("table_warm", [P, 1], F32)
        nc.scalar.activation(out=table_warm[:], in_=ident_f[:, 0:1], func=ACT.Tanh)

        laid, codes, scales = {}, {}, {}

        def make_room(key, tag, bufs, width):
            tile = ring.tile([P, width], BF16, name=tag, tag=tag, bufs=bufs, align_bytes=64)
            laid[key] = tile[:]

        def quant(key):
            words = laid[key].shape[1] // PACK
            code_tile = kept("c_%s%d%d" % key, [P, words], U32)
            scale_tile = kept("s_%s%d%d" % key, [P, words], U8)
            nc.vector.quantize_mx(out=code_tile[:].bitcast(FP8X4), scales=scale_tile[:], in_=laid[key])
            codes[key], scales[key] = code_tile[:], scale_tile[:]

        def weight_room(key):
            make_room(key, "laid", 5, KP * PACK)

        def handover_room(key):
            make_room(key, "handover", 1, KP * PACK)

        def pool_copy(out, in_):
            nc.gpsimd.tensor_scalar(out=out, in0=in_, scalar1=1.0, scalar2=0.0, op0=ALU.mult, op1=ALU.add)

        def lay_v(key, copy, lo=0, hi=NQ):
            copy(out=laid[key].rearrange("p (t q i j) -> p q t i j", t=PACK, i=RUN, j=PACK)[:, lo:hi],
                 in_=raw[key].rearrange("p j (q t i) -> p q t i j", t=PACK, i=RUN)[:, lo:hi])

        def lay_u(key, copy, lo=0, hi=NQ):
            cols = slice(lo * RUN * PACK, hi * RUN * PACK)
            copy(out=laid[key].rearrange("p (c j) -> p c j", j=PACK)[:, cols], in_=raw[key].rearrange("p j c -> p c j")[:, cols])

        def lay_u_on_scalar(key):
            nc.scalar.copy(out=laid[key].rearrange("p (c n j) -> p c j n", n=NEAR, j=PACK),
                           in_=raw[key].rearrange("p j (c n) -> p c j n", n=NEAR))

        def lay_u_on_tensor(key):
            weight_room(key)
            src = raw[key].rearrange("p j c -> p c j")
            for part in range(2):
                streamed = bank("turn", [P, 2 * KP], BF16)
                for k in range(2):
                    c0 = (2 * part + k) * P
                    nc.tensor.matmul(out=streamed[:, k * KP:(k + 1) * KP].rearrange("p (c j) -> p c j", j=PACK), lhsT=ident_b[:],
                                     rhs=src[:, c0:c0 + P, :], start=True, stop=True)
                nc.scalar.copy(out=laid[key][:, part * 2 * KP:(part + 1) * 2 * KP].bitcast(F32), in_=streamed[:].bitcast(F32))

        def turn_words(rows):
            words = rows.bitcast(F32)
            turned = bank("product", [P, NH * 2, P], F32)
            for g in range(NH):
                for w in range(2):
                    nc.tensor.transpose(turned[:, 2 * g + w, :], words[:, 256 * g + w:256 * (g + 1):2], ident_f[:])
            return turned

        def x_turn(bt):
            turned = turn_words(xl_sb[bt // 2][:, bt % 2, :])
            make_room(("x", bt, 0), "x_laid", NT, NH * KP)
            nc.scalar.copy(out=laid["x", bt, 0].bitcast(F32).rearrange("p (g b w) -> p g b w", g=NH, w=2),
                           in_=turned[:].rearrange("p (g w) b -> p g b w", w=2))

        gw_cols = kept("gw_cols", [P, E, NH, PACK], BF16)

        def gate_turn():
            turned = turn_words(small_rows[:])
            nc.scalar.copy(out=gw_cols[:].rearrange("p e g t -> p e (g t)").bitcast(F32), in_=turned[:, :, 0:E].rearrange("p w e -> p e w"))

        s_sorted = kept("s_sorted", [P, PACK, P], F32)
        gains = bank("gain", [P, PACK, P], F32)

        def gain_sort():
            nc.scalar.copy(out=s_sorted[:].rearrange("e t (q i) -> e t q i", i=RUN),
                           in_=small_rows[:, 0:R].rearrange("e (q t i) -> e t q i", t=PACK, i=RUN))

        def gain_turn():
            for t in range(PACK):
                nc.tensor.transpose(gains[:, t, :], s_sorted[:, t, :], ident_f[:])

        tanh_h, p_laid = {}, {}

        def hidden(e, bt):
            hb = bank("product", [P, PACK, P], F32)
            for t in range(PACK):
                for g in range(NH):
                    nc.tensor.matmul_mx(out=hb[:, t, :],
                                        lhsT=codes["v", e, g][:, t * P:(t + 1) * P].bitcast(FP8X4), lhsT_scale=scales["v", e, g][:, t * P:(t + 1) * P],
                                        rhs=codes["x", bt, 0][:, g * P:(g + 1) * P].bitcast(FP8X4), rhs_scale=scales["x", bt, 0][:, g * P:(g + 1) * P],
                                        start=(g == 0), stop=(g == NH - 1))
            if bt == 0:
                tanh_h[e] = ring.tile([P, B, PACK], F32, name="tanh_h", tag="tanh_h", align_bytes=64)
            nc.scalar.activation(out=tanh_h[e][:, bt * P:(bt + 1) * P, :], in_=hb[:].rearrange("p t b -> p b t"), func=ACT.Tanh)

        def gain(e, pair):
            if pair == 0:
                p_laid[e] = ring.tile([P, B * PACK], BF16, name="p_laid", tag="p_laid", align_bytes=64)
            laid["p", e, pair] = p_laid[e][:, pair * 2 * KP:(pair + 1) * 2 * KP]
            nc.vector.tensor_tensor(out=laid["p", e, pair].rearrange("p (b t) -> p b t", t=PACK),
                                    in0=tanh_h[e][:, pair * 2 * P:(pair + 1) * 2 * P, :],
                                    in1=gains[:, :, E + e:E + e + 1].rearrange("p t o -> p o t").to_broadcast([P, 2 * P, PACK]), op=ALU.mult)

        logit = bank("gate", [P, NT, E], F32)
        logit_steps = [(bt, n) for bt in range(NT) for n in range(NH * PACK)]
        top = kept("top", [P, NT], F32)
        shifted = kept("shifted", [P, NT, E], F32)
        total = kept("total", [P, NT], F32)
        inverse = kept("inverse", [P, NT], F32)
        gate = kept("gate", [P, NT, E], F32)

        def logits(steps):
            for bt, n in steps:
                g, t = divmod(n, PACK)
                x_cols = laid["x", bt, 0].rearrange("p (g b t) -> p g b t", g=NH, t=PACK)
                nc.tensor.matmul(out=logit[:, bt, :], lhsT=x_cols[:, g, :, t], rhs=gw_cols[:, :, g, t], start=(n == 0), stop=(n == NH * PACK - 1))

        def gate_max():
            nc.vector.tensor_reduce(out=top[:], in_=logit[:], axis=AX.X, op=ALU.max)

        def gate_exp():
            nc.vector.tensor_tensor(out=shifted[:], in0=logit[:], in1=top[:].unsqueeze(2).to_broadcast([P, NT, E]), op=ALU.subtract)
            nc.scalar.activation(out=shifted[:], in_=shifted[:], func=ACT.Exp)

        def gate_sum():
            nc.vector.tensor_reduce(out=total[:], in_=shifted[:], axis=AX.X, op=ALU.add)

        def gate_inverse():
            nc.vector.reciprocal(out=inverse[:], in_=total[:])

        def gate_scale():
            nc.vector.tensor_tensor(out=gate[:], in0=shifted[:], in1=inverse[:].unsqueeze(2).to_broadcast([P, NT, E]), op=ALU.mult)

        acc = {}
        for h in range(NH):
            for pair in range(2):
                acc[h, pair] = kept("acc%d%d" % (h, pair), [P, 2, KP], F32)

        def tiles_of(by_pair, bts):
            return by_pair[:, bts[0] % 2:bts[-1] % 2 + 1, :]

        def mix(e, h, bt):
            qb = bank("product", [P, KP], F32)
            span = slice((bt % 2) * P, (bt % 2 + 1) * P)
            nc.tensor.matmul_mx(out=qb[:], lhsT=codes["p", e, bt // 2][:, span].bitcast(FP8X4), lhsT_scale=scales["p", e, bt // 2][:, span],
                                rhs=codes["u", e, h].bitcast(FP8X4), rhs_scale=scales["u", e, h], start=True, stop=True)
            dst = acc[h, bt // 2][:, bt % 2, :]
            if e == 0:
                nc.scalar.activation(out=dst, in_=qb[:], func=ACT.Copy, scale=gate[:, bt, 0:1])
            else:
                nc.vector.scalar_tensor_tensor(out=dst, in0=qb[:], scalar=gate[:, bt, e:e + 1], in1=dst, op0=ALU.mult, op1=ALU.add)

        def times_x0(h, bts):
            dst = tiles_of(acc[h, bts[0] // 2], bts)
            nc.vector.tensor_tensor(out=dst, in0=dst, in1=tiles_of(x0_sb[bts[0] // 2], bts)[:, :, h * KP:(h + 1) * KP], op=ALU.mult)

        def plus_xl(h, bt, engine):
            dst = acc[h, bt // 2][:, bt % 2, :]
            engine.tensor_tensor(out=dst, in0=dst, in1=xl_sb[bt // 2][:, bt % 2, h * KP:(h + 1) * KP], op=ALU.add)
            nc.sync.dma_start(out=out_0[bt * P:(bt + 1) * P, h * KP:(h + 1) * KP], in_=dst)

        rounded_words = {}

        def out_round(h, bts):
            rounded = ring.tile([P, len(bts), 2, P, 2], BF16, name="rounded", tag="rounded", align_bytes=64)
            nc.scalar.copy(out=rounded[:], in_=tiles_of(acc[h, bts[0] // 2], bts).rearrange("b n (p w i) -> b n w p i", w=2, i=2))
            rounded_words[h, bts] = rounded[:].rearrange("b n w p i -> b (n w p i)").bitcast(F32)

        def out_turn(h, bts):
            n = len(bts)
            turned = bank("turn", [P, n, 2, P], F32)
            for k in range(n):
                for w in range(2):
                    nc.tensor.transpose(turned[:, k, w, :], rounded_words[h, bts][:, (2 * k + w) * P:(2 * k + w + 1) * P], ident_f[:])
            make_room(("o", h, bts), "out_laid", 3, n * KP)
            nc.scalar.copy(out=laid["o", h, bts].bitcast(F32).rearrange("p (n b w) -> p n b w", n=n, w=2),
                           in_=turned[:].rearrange("p n w b -> p n b w"))

        out_scales = [kept("out_scales%d" % h, [P, B], U8) for h in range(NH)]

        def out_quant(h, bts):
            span = slice(bts[0] * P, (bts[-1] + 1) * P)
            words = kept("out_words%d%d" % (h, bts[0]), [P, len(bts) * P], I32)
            nc.vector.quantize_mx(out=words[:].bitcast(FP8X4), scales=out_scales[h][:, span], in_=laid["o", h, bts])
            nc.sync.dma_start(out=out_1[h].rearrange("p m t -> p (m t)").bitcast(I32)[:, span], in_=words[:])
            if bts[-1] == NT - 1:
                for n in range(P // 32):
                    queue = nc.scalar if (h == NH - 1 and n % 2) else nc.sync
                    queue.dma_start(out=out_2[h, 4 * n:4 * n + 4, :].bitcast(I32), in_=out_scales[h][32 * n:32 * n + 4, :].bitcast(I32))

        def lay_v_on_vector(e, g):
            weight_room(("v", e, g))
            lay_v(("v", e, g), nc.vector.tensor_copy)

        lay_v_on_vector(0, 0)
        x_turn(0)
        x_turn(1)
        quant(("v", 0, 0))
        lay_v_on_vector(0, 1)
        quant(("x", 0, 0))
        quant(("v", 0, 1))
        quant(("x", 1, 0))
        x_turn(2)
        lay_v_on_vector(1, 0)
        hidden(0, 0)
        gain_sort()
        hidden(0, 1)
        quant(("x", 2, 0))
        x_turn(3)
        hidden(0, 2)
        handover_room(("v", 2, 0))
        lay_v(("v", 2, 0), nc.scalar.copy, NQ // 2, NQ)
        lay_v_on_vector(1, 1)
        quant(("v", 1, 0))
        quant(("x", 3, 0))
        hidden(0, 3)
        gain_turn()
        lay_v(("v", 2, 0), nc.vector.tensor_copy, 0, NQ // 2)
        gate_turn()
        quant(("v", 1, 1))
        quant(("v", 2, 0))

        on_pool = [("v", 2, 1), ("v", 3, 1), ("u", 2, 0), ("u", 3, 0)]
        on_scalar = [("v", 3, 0), ("u", 0, 0), ("u", 1, 0)]
        gate_round = 2
        for e in range(E):
            handover_room(on_pool[e])
            lay = lay_v if on_pool[e][0] == "v" else lay_u
            lay(on_pool[e], pool_copy, 0, POOL_BLOCKS)
            gain(e, 0)
            if e == gate_round:
                gate_max()
            gain(e, 1)
            if e == gate_round:
                gate_exp()
            if e + 1 < E:
                for bt in range(NT):
                    hidden(e + 1, bt)
                    first = (e * NT + bt) * LOGITS_PER_TILE
                    logits(logit_steps[first:first + LOGITS_PER_TILE])
                weight_room(on_scalar[e])
                if on_scalar[e][0] == "v":
                    lay_v(on_scalar[e], nc.scalar.copy)
                else:
                    lay_u_on_scalar(on_scalar[e])
            else:
                rotation["product"] = rotation["product"] + rotation["gate"] + rotation["gain"]
                for bt in range(NT):
                    mix(0, 0, bt)
                lay_u_on_tensor(("u", 1, 1))
            lay(on_pool[e], nc.vector.tensor_copy, POOL_BLOCKS, NQ)
            quant(("p", e, 0))
            if e == gate_round:
                gate_sum()
            quant(("p", e, 1))
            if e == gate_round:
                gate_inverse()
            if e > 0:
                quant(on_scalar[e - 1])
            if e == gate_round:
                gate_scale()
            quant(on_pool[e])
        handover_room(("u", 0, 1))
        lay_u(("u", 0, 1), pool_copy)

        units = [(h, (2 * pair, 2 * pair + 1)) for h in range(NH) for pair in range(2)]
        last = len(units) - 1
        for k, (h, bts) in enumerate(units):
            for e in range(1, E):
                for bt in bts:
                    mix(e, h, bt)
                if e == 2 and k == 1:
                    lay_u_on_tensor(("u", 3, 1))
                if e == 2 and k >= 2:
                    out_turn(*units[k - 2])
            if k == 0:
                quant(("u", 1, 1))
                lay_u_on_tensor(("u", 2, 1))
            if k == 1:
                for e in (0, 2, 3):
                    quant(("u", e, 1))
            if 0 < k < last:
                for bt in units[k + 1][1]:
                    mix(0, units[k + 1][0], bt)
            if k >= 1:
                out_round(*units[k - 1])
            if k >= 2:
                out_quant(*units[k - 2])
            if k < last:
                times_x0(h, bts)
                for bt in bts:
                    plus_xl(h, bt, nc.gpsimd)
            else:
                out_turn(*units[k - 1])
                for bt in bts:
                    times_x0(h, (bt,))
                for bt in bts:
                    plus_xl(h, bt, nc.vector)
                    out_round(h, (bt,))
                for bt in bts:
                    out_turn(h, (bt,))
                out_quant(*units[k - 1])
                for bt in bts:
                    out_quant(h, (bt,))
